import numpy as np, ml_dtypes
CORES = [25,29,65,69,153,157,193,197]
N = 8
import mx_ref
BF = ml_dtypes.bfloat16
def cols(t, e):
    v = np.concatenate([t.reshape(128, -1, 4), np.zeros((128, 1, 4), BF)], axis=1)
    return np.ascontiguousarray(v[:, e]).reshape(128, -1)
def cut(t, i, w=512):
    return t[:, w * i:w * i + w]
def tile(rs):
    return np.stack(rs, axis=2).reshape(128, -1).astype(BF)
def pick(q, e):
    c = np.concatenate([q[0].reshape(128, -1, 4), np.zeros((128, 1, 4), np.uint8)], axis=1); s = np.concatenate([q[1], np.ones((16, 1), np.uint8)], axis=1)
    return (np.ascontiguousarray(c[:, e].reshape(128, -1)), np.ascontiguousarray(s[:, e]))
def join(*qs):
    return (np.concatenate([q[0] for q in qs], axis=1), np.concatenate([q[1] for q in qs], axis=1))
def put(q, e, v):
    c, s = q[0].reshape(128, -1, 4).copy(), q[1].copy(); c[:, e] = v[0].reshape(128, -1, 4); s[:, e] = v[1]
    return (c.reshape(128, -1), s)
def pk(c, s):
    return (np.ascontiguousarray(c), mx_ref.live(s))
def emit(q):
    return q[0], q[1]
def decode(q):
    o = []
    for b in range(4):
        e = np.zeros((128, 128, 4), np.float32); e[np.arange(128), np.arange(128), b] = 1
        o.append(mx_ref.matmul(mx_ref.quantize(e.reshape(128, 512).astype(BF)), q))
    return np.stack(o, axis=2).reshape(128, -1)
def f(rng, *shape):
    return mx_ref.flush((rng.standard_normal(shape, dtype=np.float32) * np.exp2(rng.integers(-2, 3, shape[:-1] + (1,)))).astype(BF))
def wide(rng, *shape, cols=0):
    v = rng.standard_normal(shape, dtype=np.float32) * np.exp2(rng.integers(-12, 13, shape)).astype(np.float32)
    if cols: v *= np.repeat(np.exp2(rng.integers(-cols, cols + 1, shape[:-2] + (1, shape[-1] // 4))) * (rng.random(shape[:-2] + (1, shape[-1] // 4)) > 0.0625), 4, axis=-1).astype(np.float32)
    return mx_ref.flush(v.astype(BF))
T, CAPP, CAPR = 128, 48, 16
def big(v, k):
    v = v.astype(np.float32) * np.float32(k)
    v[np.abs(v) < np.float32(2.0 ** -6)] = 0
    return v.astype(BF)
def same(t):
    return np.repeat(t[None], N, axis=0)
def only(t, k):
    t = np.array(t)
    t[:, 4 * k:] = 0
    return t
def plain(rng):
    return {"x": f(rng, N, 128, 4 * T), "gr": big(f(rng, N, 128, 4 * T), 8), "rt": same(only(f(rng, 128, 512), N)), "w": f(rng, N, 128, 2048), "ub": big(f(rng, N, 128, 2048), 4), "pr": same(only(f(rng, 128, 512), 1)), "v": f(rng, N, 128, 512)}
def deal(rng, n, among):
    m, j, p = len(among), np.arange(n), rng.permutation(among)
    return np.stack([p[j % m], p[(j + 1 + j // m % (m - 1)) % m]], axis=1)
def routed(rng, to, far=False):
    g = np.arange(128) // (128 // N)
    rt = np.zeros((128, 128, 4), np.float32)
    rt[np.arange(128), g, 0] = 1 + rng.random(128)
    x = rng.standard_normal((N, 128, T, 4)) * (2 if far else 8)
    low = 0.125 * rng.choice([-1.0, 1.0], (N, 128, T))
    first, second = to[:, None, :, 0] == g[None, :, None], to[:, None, :, 1] == g[None, :, None]
    size = np.where(first, low, np.where(second, -4.0, -16.0)) if far else np.where(first, 16.0, np.where(second, 2.0, low))
    x[..., 0] = size * (1 + rng.random((N, 128, T)))
    if far: x, rt = x * 2.0 ** 25, rt * np.float32(2.0 ** 29)
    return {"x": mx_ref.flush(x.reshape(N, 128, 4 * T).astype(np.float32).astype(BF)), "rt": same(rt.reshape(128, 512).astype(BF))}
def setup_inputs(rng):
    return plain(rng)
def setup_inputs_crowd(rng):
    h = int(rng.integers(0, N))
    rest, n, to = np.delete(np.arange(N), h), [CAPP, T, CAPP + 1, CAPR, 0, CAPR + 1, CAPR - 1, 1], np.zeros((N, T, 2), int)
    for i in range(N):
        t = deal(rng, T, rest)
        t[np.arange(n[i]), rng.integers(0, 2, n[i])] = h
        to[(h + 1 + i) % N] = t[rng.permutation(T)]
    d = {**plain(rng), **routed(rng, to)}
    sign, pr = rng.choice([-1.0, 1.0], (128, 1, 4)), np.zeros((128, 128, 4), np.float32)
    pr[:, :1] = 2.0 ** 29 * sign * (1 + rng.random((128, 1, 4)))
    gr = 2.0 ** 28 * sign[None] * (1 + rng.random((N, 128, T, 4))) * rng.choice([-1.0, 1.0], (N, 1, T, 1))
    d["pr"] = same(pr.reshape(128, 512).astype(BF))
    d["gr"] = gr.reshape(N, 128, 4 * T).astype(np.float32).astype(BF)
    d["ub"] = (d["ub"].astype(np.float32) * np.float32(2.0 ** -22)).astype(BF)
    return d
def setup_inputs_dead(rng):
    rest = np.delete(np.arange(N), int(rng.integers(0, N)))
    to, dead = np.zeros((N, T, 2), int), np.zeros((N, T), bool)
    for q in range(N):
        s = rng.permutation(T)
        to[q] = deal(rng, T, rest)[s]
        dead[q] = s // (N - 1) % 4 != 0
    d = {**plain(rng), **routed(rng, to)}
    x = d["x"].astype(np.float32).reshape(N, 128, T, 4)
    x[..., 1:] = 16 * (1 + rng.random((N, 128, T, 3))) * np.where(dead, 1.0, -1.0)[:, None, :, None]
    d["x"] = x.reshape(N, 128, 4 * T).astype(BF)
    w = np.array(d["w"])
    w[rng.permutation(rest)[:N // 2]] = (-1 - rng.random((N // 2, 128, 2048))).astype(np.float32).astype(BF)
    d["w"] = w
    return d
def setup_inputs_one(rng):
    h = int(rng.integers(0, N))
    to = np.full((N, T, 2), h)
    for q in range(N): to[q, :, 1] = rng.permutation(deal(rng, T, np.delete(np.arange(N), h))[:, 0])
    return {**plain(rng), **routed(rng, to, far=True)}
def setup_inputs_spread(rng):
    d = plain(rng)
    x = (wide(rng, N, 128, 4 * T, cols=6).astype(np.float32) * np.float32(2.0 ** 8)).reshape(N, 128, T, 4)
    for q in range(N):
        i = rng.permutation(T)[:T // 8]
        x[q][:, i] = 2.0 ** -29 * (1 + rng.random((128, i.size, 4))) * rng.choice([-1.0, 1.0], (128, i.size, 4))
    d["x"] = x.reshape(N, 128, 4 * T).astype(BF)
    d["rt"] = (d["rt"].astype(np.float32) * np.float32(2.0 ** 20)).astype(BF)
    d["gr"] = big(wide(rng, N, 128, 4 * T, cols=3), 16)
    return d
def setup_inputs_ties(rng):
    u, o = sorted(rng.permutation(N)[:2].tolist())
    rest = np.delete(np.arange(N), [u, o])
    to, at = np.zeros((N, T, 2), int), []
    for q in range(N):
        t, s = deal(rng, T, rest), rng.permutation(T)
        t[:T // 2] = np.array([u, rest[0]])
        t[T // 2:T // 2 + 4, 1] = u
        to[q] = t[s]
        at.append(np.flatnonzero(s < T // 2))
    d = {**plain(rng), **routed(rng, to)}
    r = np.array(d["rt"]).reshape(N, 128, 128, 4)
    r[:, :, o] = r[:, :, u]
    x, g = d["x"].astype(np.float32).reshape(N, 128, T, 4), d["gr"].astype(np.float32).reshape(N, 128, T, 4)
    for q in range(N):
        i = at[q]
        x[q][:, i] = x[q][:, i[:1]].copy()
        g[q][:, i] = g[q][:, i[:1]].copy() * rng.choice([-1.0, 1.0], i.size)[None, :, None]
    return {**d, "x": x.reshape(N, 128, 4 * T).astype(BF), "gr": g.reshape(N, 128, 4 * T).astype(BF), "rt": r.reshape(N, 128, 512)}
def check_inputs(d):
    b = []
    for k in ("x", "gr", "rt", "w", "ub", "pr", "v"):
        a = np.abs(d[k].astype(np.float32))
        if not (np.isfinite(a).all() and ((a == 0) | (a >= 2.0 ** -30) & (a <= 2.0 ** 30)).all()): b.append("a value of " + k)
    for k, n in (("rt", N), ("pr", 1)):
        a = d[k].astype(np.float32)
        if (a != a[:1]).any(): b.append(k + " differs between ranks")
        if (a[:, :, 4 * n:] != 0).any(): b.append(k + " has numbers behind its first columns")
    return b
def reference(x, gr, rt, w, ub, pr, v):
    qz = lambda t: mx_ref.quantize(np.ascontiguousarray(t))
    to = []
    for q in range(N):
        s = mx_ref.matmul(qz(rt[q]), qz(x[q]))[:N] + np.float32(0)
        to.append(np.argsort(-s, axis=0, kind="stable")[:2])
    everyx, everyg = np.concatenate([x[q] for q in range(N)], axis=1), np.concatenate([gr[q] for q in range(N)], axis=1)
    came = np.zeros((N, 128, 2 * T, 4), np.float32)
    ct = np.zeros((N, 1, T), np.float32)
    for e in range(N):
        taken = [np.flatnonzero((to[q] == e).any(axis=0))[:CAPP] for q in range(N)]
        at = np.full((N, CAPP), -1)
        for q in range(N): at[q, :taken[q].size] = T * q + taken[q]
        at = at.reshape(-1)
        xs, gs = qz(cols(everyx, at)), qz(cols(everyg, at))
        forward = np.stack([mx_ref.matmul(qz(cut(w[e], i)), xs) for i in range(4)], axis=2).reshape(128, -1)
        m = qz(np.where(forward > 0, decode(gs), np.float32(0)).astype(BF))
        strength = np.abs(mx_ref.matmul(qz(pr[e]), m)[0])
        dx = decode(qz(tile([mx_ref.matmul(qz(cut(ub[e], i)), m) * np.float32(0.0625) for i in range(4)]))).reshape(128, -1, 4)
        for q in range(N):
            k = np.argsort(-strength[CAPP * q:CAPP * q + taken[q].size], kind="stable")[:CAPR]
            j = taken[q][k]
            second = (to[q][1, j] == e).astype(int)
            came[q][:, T * second + j] = dx[:, CAPP * q + k]
            ct[q, 0, j] += 1 + second
    oc, osc, y = np.zeros((N, 128, 4 * T), np.uint8), np.zeros((N, 16, T), np.uint8), np.zeros((N, 128, T), np.float32)
    for q in range(N):
        z = qz((came[q][:, :T] + came[q][:, T:]).reshape(128, 4 * T).astype(BF))
        oc[q], osc[q] = emit(z)
        y[q] = mx_ref.matmul(qz(v[q]), z)
    return {"oc": oc, "osc": osc, "ct": ct, "y": y}

@@ -1,0 +1,452 @@
+from concourse.bass import DstId, RemoteDMATransfer
+from concourse.mybir import dt, AluOpType, AxisListType, ActivationFunctionType
+
+OP, AX, AF = AluOpType, AxisListType, ActivationFunctionType
+N, CAPP, CAPR = 8, 48, 16
+SIM = 256
+BIG = 9.0e29
+NS = 8
+
+F8, U8, U16, BF, F32, I32 = "float8_e4m3fn_x4", "uint8", "uint16", "bfloat16", "float32", "int32"
+SCRATCH = {}
+for _n, _w in dict(xin=512, grin=512, rtin=512, win=2048, ubin=2048, prin=512, vin=512, zt=512, e4=2048, kt=1024,
+                   cb=2048, jk=2048, rsw=512, gg=256, gt=256, zz=512, bign=2816, bigc=2816).items():
+    SCRATCH[_n] = ("sbuf", [128, _w], BF)
+for _n, _w in dict(own=512, rt=128, rp=128, ww=512, uu=512, pp=128, pq=128, vv=128, ee=512, kk=256, pk=768, hd=96, hr=16, cam=256,
+                   zp=256, zq=128, lxn=192, lgn=192, mmn=192, ddn=192, ohn=128, rrn=64, lxc=192, lgc=192, mmc=192, ddc=192, ohc=128, rrc=64).items():
+    SCRATCH[_n + "c"] = ("sbuf", [128, _w], F8)
+    SCRATCH[_n + "s"] = ("sbuf", [128, _w], U8)
+for _n, _w in dict(off=48, offg=16, fo=16, hrl=2, lland=8, pon=4, poc=4, lln=4, llc=4).items():
+    SCRATCH[_n] = ("sbuf", [128, _w], U16)
+for _n, _w in dict(st=160, fn=512, fc=512, yo=128).items():
+    SCRATCH[_n] = ("sbuf", [128, _w], F32)
+for _i in range(8):
+    SCRATCH["ps%d" % _i] = ("psum", [128, 512], F32)
+VIEW = {}
+for _b, _d, _l in (("ii", I32, "ip8 ic8 ra8 ta8 tb8 ua8 ub8 uc8 ud8 sa8 sb8 sc8 ka8 kb8 kq8 ea8 eb8 ec8 ed8 ef8"),
+                   ("lu", U16, "la8 lb8 lc8 ld8"),
+                   ("kf", F32, "kcol8 kdol8 kthr8 kr16 kk16 nk16 kx48 cse32 rs32"),
+                   ("kb", BF, "vals128 its128 idn128 ones128 wn96 wm96"),
+                   ("df", F32, "xd32 xo32 va32 vb32 iab64 vab64 vac32 vad16 vae8 xa16 pfa32 pra32 pfb32 prb32 vf40 vr40"),
+                   ("db", BF, "fb128 ft128 cum128 ctr128 nla32 nlb32 nra32 nrb32 nl32 nr32 np32"),
+                   ("hf", F32, "cf32 cft32 cfa8 cfb8")):
+    _o = 0
+    for _t in _l.split():
+        _n = _t.rstrip("0123456789")
+        VIEW[_n] = (_b, _o, int(_t[len(_n):]))
+        _o += int(_t[len(_n):])
+    SCRATCH[_b] = ("sbuf", [128, _o], _d)
+
+SEMAPHORES = ["vq", "sq", "tq", "gq", "ldx", "ldrt", "ldgr", "ldpr", "ldw", "ldu", "ldv", "selfcp", "outs", "outs2", "loc",
+              "hci", "hsi", "hli", "hri", "hrsi", "cco", "csc", "nco", "nsc", "rlc", "rcc", "rsc", "rln", "rcn", "rsn"]
+
+
+def roads(T, topo):
+    cores = [int(c) for c in T.cores]
+    cross = [[e for e in range(N) if e != q and not topo.may_write(cores[q], cores[e])] for q in range(N)]
+    road = {}
+    for q in range(N):
+        for e in cross[q]:
+            cq, ce = cores[q], cores[e]
+            if topo.die(cq) == topo.die(ce):
+                hs = [h for h in topo.cores_of(cq) if h != cq and topo.die(h) == topo.die(cq) and topo.may_write(h, ce)]
+                k = [f for f in cross[q] if topo.die(cores[f]) == topo.die(cq)].index(e)
+            else:
+                hs = [h for h in range(SIM) if topo.mates(h, ce) and topo.die(h) == topo.die(ce) and topo.may_write(cq, h) and topo.may_write(h, ce)]
+                k = [s for s in cross[e] if topo.die(cores[s]) != topo.die(ce)].index(q)
+            road[(q, e)] = hs[k % len(hs)]
+    return cores, cross, road
+
+
+def bits(es):
+    return sum(1 << e for e in es)
+
+
+def by(v):
+    return v.bitcast(dt.uint8)
+
+
+def w4(v):
+    return v.bitcast(dt.uint32)
+
+
+def hand_on(g, core, T, topo):
+    cores, cross, road = roads(T, topo)
+    mine = [k for k, h in road.items() if h == core]
+    if not mine:
+        return
+    q, e = mine[0]
+    ce = cores[e]
+    rid, pid = topo.addr(ce, core)
+    es = topo.engines(core, ce)
+    al, hs = bits(es), (bits(es[:len(es) // 2]), bits(es[len(es) // 2:]))
+    k = cross[e].index(q)
+    a = k * CAPP
+
+    def two(sem, srcs, dsts):
+        g.remote_dma_fused([RemoteDMATransfer(dst_ids=[DstId(rid=rid, pnc=pid)], dma_engine_mask=m, remote_sem=T.sem[sem], src=s, dst=d)
+                            for m, s, d in zip(hs, srcs, dsts)], local_sem=T.sem.loc)
+    g.wait_ge(T.sem.hci, 4)
+    two("cco", [by(T.hdc[:, 0:48]), by(T.hdc[:, 48:96])], [by(T.lxcc[:, a:a + 48]), by(T.lgcc[:, a:a + 48])])
+    g.wait_ge(T.sem.hsi, 4)
+    two("csc", [T.hds[:, 0:48], T.hds[:, 48:96]], [T.lxcs[:, a:a + 48], T.lgcs[:, a:a + 48]])
+    a = 16 * k
+    for sem, rsem, src, to in (("hli", "rlc", T.hrl[:, 0:1], T.lland[:, k:k + 1]),
+                               ("hri", "rcc", by(T.hrc[:]), by(T.camc[:, a:a + 16])),
+                               ("hrsi", "rsc", T.hrs[:], T.cams[:, a:a + 16])):
+        g.wait_ge(T.sem[sem], 4)
+        g.remote_dma(to, src, T.sem[rsem], T.sem.loc, pid, rid, al)
+    g.wait_ge(T.sem.loc, 5 * len(es))
+
+
+def rank_program(g, core, T, topo):
+    me = T.rank_of(core)
+    if me is None:
+        return hand_on(g, core, T, topo)
+    cores, cross_all, road = roads(T, topo)
+    cross = cross_all[me]
+    near_of = lambda r: [s for s in range(N) if s != r and s not in cross_all[r]]
+    near = near_of(me)
+    onchip = lambda a, b: cores[b] in topo.cores_of(cores[a])
+    seat = lambda r: near_of(r)[:2] + [r] + near_of(r)[2:]
+
+    eng = {"vq": g.vector, "sq": g.scalar, "tq": g.tensor, "gq": g, "sync": g.sync}
+    cnt = {"vq": 0, "sq": 0, "tq": 0, "gq": 0}
+    seen = {q: {} for q in eng}
+
+    def wait(q, deps):
+        best = {}
+        for s, n in deps:
+            best[s] = max(best.get(s, 0), n)
+        for s, n in best.items():
+            if seen[q].get(s, 0) < n:
+                eng[q].wait_ge(T.sem[s], n)
+                seen[q][s] = n
+
+    def run(q, deps, fn, *a, **k):
+        wait(q, deps)
+        fn(*a, **k).then_inc(T.sem[q], 1)
+        cnt[q] += 1
+        return (q, cnt[q])
+
+    calls = {"copy": g.vector.tensor_copy, "tt": g.vector.tensor_tensor, "ts": g.vector.tensor_scalar, "red": g.vector.tensor_reduce,
+             "scan": g.vector.tensor_tensor_scan, "tr": g.vector.transpose, "set": g.vector.memset, "q": g.vector.quantize_mx}
+    V = lambda deps, name, *a, **k: run("vq", deps, calls[name], *a, **k)
+    S = lambda deps, *a, **k: run("sq", deps, g.scalar.activation, *a, **k)
+    G = lambda deps, fn, *a, **k: run("gq", deps, fn, *a, **k)
+    MM = lambda deps, out, l, r, a, b: run("tq", deps, g.tensor.matmul_mx, out, l[0], l[1], r[0], r[1], a, b)
+    used = [[] for _ in range(8)]
+    PS = [T["ps%d" % i] for i in range(8)]
+
+    def C(n, a=0, b=None, st=1):
+        buf, s, w = VIEW[n]
+        b = w if b is None else b
+        return T[buf][:, s + a:s + b] if st == 1 else T[buf][:, s + a:s + b:st]
+
+    def qp(n, a=0, b=None):
+        c, s = T[n + "c"], T[n + "s"]
+        b = c.shape[1] if b is None else b
+        return c[:, a:b], s[:, a:b]
+
+    def quant(deps, n, a, b, tile):
+        c, s = qp(n, a, b)
+        return V(deps, "q", c, s, tile)
+
+    def pickq(deps, to, frm, o):
+        return V(deps, "copy", w4(to[0]), w4(frm[0]).indirect(o)), S(deps, to[1], frm[1].indirect(o), AF.Copy)
+
+    def load(q, sem, out, in_):
+        q.dma_start(out, in_).then_inc(T.sem[sem], 16)
+        return (sem, 16)
+    lx = load(g.sync, "ldx", T.xin[:], T.x[:])
+    lrt = load(g.scalar, "ldrt", T.rtin[:], T.rt[:])
+    lgr = load(g.sync, "ldgr", T.grin[:], T.gr[:])
+    lw = load(g.scalar, "ldw", T.win[:], T.w[:])
+    lpr = load(g.sync, "ldpr", T.prin[:], T.pr[:])
+    lu = load(g.sync, "ldu", T.ubin[:], T.ub[:])
+    lv = load(g.scalar, "ldv", T.vin[:], T.v[:])
+
+    iota = lambda n, pat, base, cm: G([], g.iota, C(n), pat, base, cm, allow_small_or_imprecise_dtypes=True)
+    gip = G([], g.iota, C("ip"), [[0, 8]], 0, 1)
+    gic = G([], g.iota, C("ic"), [[16, 8]], 0, 0)
+    gkr = iota("kr", [[1, 16]], 0, 0)
+    gcs = iota("cse", [[0, 4], [64, 8]], -1, 0)
+    gk48 = iota("kx", [[1, 48]], 0, 0)
+    gi2 = iota("its", [[0, 8], [2, 16]], -48, 0)
+    gva = iota("vals", [[1, 128]], 0, 0)
+    vz = V([], "set", T.zt[:], 0.0)
+    vone = V([], "set", C("ones"), 1.0)
+    vr1 = V([], "set", C("rs"), BIG)
+    vs1 = V([], "set", T.st[:, 0:32], 0.0)
+    vs2 = [V([], "set", C(n, 0, 8), 0.0) for n in ("vf", "vr")][1]
+    ra = V([gip], "ts", C("ra"), C("ip"), 15, None, OP.bitwise_and)
+    vr2 = V([vr1], "set", C("rs", 0, 32, 8), -BIG)
+    ua = V([ra], "ts", C("ua"), C("ra"), 7, None, OP.bitwise_and)
+    sa = V([ra], "ts", C("sa"), C("ra"), 2, None, OP.logical_shift_right)
+    sb = V([gic], "ts", C("sb"), C("ic"), 2, None, OP.logical_shift_right)
+    ea = V([gic], "ts", C("ea"), C("ic"), 16, 2, OP.bitwise_and, OP.logical_shift_right)
+    ta = V([ra], "ts", C("ta"), C("ra"), 3, None, OP.bitwise_and)
+    ub = V([ua], "ts", C("ub"), C("ua"), -2, 7, OP.mult, OP.add)
+    eb = V([ea, sa], "tt", C("eb"), C("ea"), C("sa"), OP.add)
+    tb = V([ta], "ts", C("tb"), C("ta"), 1, None, OP.is_equal)
+    sc = V([sa, sb], "tt", C("sc"), C("sa"), C("sb"), OP.add)
+    ec = V([eb], "ts", C("ec"), C("eb"), -2, 7, OP.mult, OP.add)
+    ed = V([ec, tb], "tt", C("ed"), C("ec"), C("tb"), OP.mult)
+    ef = V([ed], "tt", C("ef"), C("ed"), C("eb"), OP.add)
+    l1 = V([ef], "copy", C("lb"), C("ef"))
+    uc = V([ub], "tt", C("uc"), C("ub"), C("ra"), OP.add)
+    l3 = V([sc], "copy", C("ld"), C("sc"))
+    ud = V([uc], "tt", C("ud"), C("uc"), C("ic"), OP.add)
+    kq = V([gip], "ts", C("kq"), C("ip"), 3, None, OP.bitwise_and)
+    l2 = V([ud], "copy", C("lc"), C("ud"))
+    kt = V([kq], "ts", C("kthr"), C("kq"), 16, None, OP.mult)
+    kk = V([kt, gkr], "ts", C("kk"), C("kr"), C("kthr", 0, 1), None, OP.add)
+    nk = V([kk], "ts", C("nk"), C("kk"), -1.0, -0.5, OP.mult, OP.add)
+    qz1 = quant([vz], "own", 128, 256, T.zt[:])
+    qz2 = quant([vz], "own", 384, 512, T.zt[:])
+
+    qrt = quant([lrt], "rt", 0, 128, T.rtin[:])
+    prt, prs = pickq([qrt, l1], qp("rp"), qp("rt"), C("lb"))
+    qx = quant([lx], "own", 0, 128, T.xin[:])
+    ms = MM([prt, prs, qx], PS[0][:, 0:128], qp("rp"), qp("own", 0, 128), True, True)
+    qg = quant([lgr], "own", 256, 384, T.grin[:])
+    tr = V([ms, vs1], "tr", T.st[:, 32:160], PS[0][:, 0:128])
+    used[0] = [tr]
+    X = [T.st[:, 32 + u:160:4] for u in range(2)]
+    p1 = [V([tr, vr2], "scan", C(("pfa", "pra")[u]), T.st[:, 28 + u:156:4], C("rs"), 0.0, OP.max, OP.min) for u in range(2)]
+    v3 = [V([p1[u], vs2], "tt", C(("vf", "vr")[u], 8, 40), X[u], C(("pfa", "pra")[u]), OP.min) for u in range(2)]
+    c1 = V([p1[0]], "tt", C("nla"), C("pfa"), X[0], OP.is_ge)
+    c2 = V([p1[1]], "tt", C("nra"), C("pra"), X[1], OP.is_gt)
+    p2 = [V([v3[u]], "scan", C(("pfb", "prb")[u]), C(("vf", "vr")[u], 7, 39), C("rs"), 0.0, OP.max, OP.min) for u in range(2)]
+    c4 = V([p2[0]], "tt", C("nlb"), C("pfb"), X[0], OP.is_ge)
+    c3 = V([p2[1]], "tt", C("nrb"), C("prb"), X[1], OP.is_gt)
+    a2 = V([c1, c4], "tt", C("nl"), C("nla"), C("nlb"), OP.add)
+    a1 = V([c2, c3], "tt", C("nr"), C("nra"), C("nrb"), OP.add)
+    npn = V([a1, a2, l2], "tt", C("np"), C("nr").indirect(C("lc", 0, 2)), C("nl"), OP.add)
+    fb = V([npn, l3], "ts", C("fb"), C("np").indirect(C("ld")), 1.5, None, OP.is_lt)
+    ft = V([fb], "tr", C("ft"), C("fb"))
+    cum = V([ft, vz], "scan", C("cum"), C("ft"), T.zt[:, 0:128], 0.0, OP.add, OP.add)
+    sa = None
+    for r in range(NS):
+        sa = S([cum, nk], T.jk[:, 128 * r:128 * r + 128], C("cum"), AF.Sign, bias=C("nk", r, r + 1), accum_out=C("xa", r, r + 1))
+    cmps = [V([cum, kk], "ts", T.cb[:, 128 * r:128 * r + 128], C("cum"), C("kk", r, r + 1), None, OP.is_le) for r in range(NS, 16)]
+    red = None
+    for r in range(NS, 16):
+        red = V([cmps[r - NS]], "red", C("xd", r, r + 1), T.cb[:, 128 * r:128 * r + 128], AX.X, OP.add)
+    d1 = V([red], "copy", C("xd", 16 + NS, 32), C("xd", NS, 16))
+    d2 = V([sa], "ts", C("xd", 0, NS), C("xa", 0, NS), -0.5, 64.0, OP.mult, OP.add)
+    d3 = V([sa], "ts", C("xd", 16, 16 + NS), C("xa", 0, NS), -0.5, 64.0, OP.mult, OP.add)
+    xo = V([d1, d2, d3], "tr", C("xo"), C("xd"))
+    of = None
+    for c in range(3):
+        V([xo], "copy", T.off[:, c:48:6], C("xo", c, 32, 4))
+        of = V([xo], "ts", T.off[:, 3 + c:48:6], C("xo", c, 32, 4), 256.0, None, OP.add)
+
+    def pick(es):
+        runs, r = [], None
+        for e in sorted(es):
+            if runs and runs[-1][1] == e:
+                runs[-1][1] = e + 1
+            else:
+                runs.append([e, e + 1])
+        for lo, hi in runs:
+            r = pickq([of, qz1, qz2, qx, qg], qp("pk", 96 * lo, 96 * hi), qp("own"), T.off[:, 6 * lo:6 * hi])
+        return r
+    pc, psc = pick(cross)
+    nc, nsc = pick(near + [me])
+    wait("sync", [nc, nsc])
+    k, m = 48 * 2, 96 * me
+    for out, in_ in ((by(T.lxnc[:, k:k + 48]), by(T.pkc[:, m:m + 48])), (by(T.lgnc[:, k:k + 48]), by(T.pkc[:, m + 48:m + 96])),
+                     (T.lxns[:, k:k + 48], T.pks[:, m:m + 48]), (T.lgns[:, k:k + 48], T.pks[:, m + 48:m + 96])):
+        g.sync.dma_start(out, in_).then_inc(T.sem.selfcp, 16)
+
+    offe = topo.engines(core, [cores[e] for e in near if not onchip(me, e)][0])
+    one = [x for x in topo.engines(core, [cores[e] for e in near if onchip(me, e)][0]) if x not in offe]
+    loc = [0]
+
+    def fused(trs):
+        l = []
+        for d, es, s, a, b in trs:
+            rid, pid = topo.addr(d, core)
+            l.append(RemoteDMATransfer(dst_ids=[DstId(rid=rid, pnc=pid)], dma_engine_mask=bits(es), remote_sem=T.sem[s], src=a, dst=b))
+            loc[0] += len(es)
+        g.remote_dma_fused(l, local_sem=T.sem.loc)
+
+    hop, nhop, ka, kb = {}, {}, 0, 0
+    for e in cross:
+        h = road[(me, e)]
+        if h in topo.cores_of(core):
+            hop[e], ka = (h, one[ka:ka + 4]), ka + 4
+        else:
+            hop[e], kb = (h, offe[kb:kb + 4]), kb + 4
+    kb = 0
+    for e in near:
+        if onchip(me, e):
+            nhop[e] = one
+        else:
+            nhop[e], kb = offe[kb:kb + 4], kb + 4
+    half = lambda l, i: l[len(l) // 2 * i:len(l) // 2 * (i + 1)]
+
+    wait("gq", [pc])
+    fused([(*hop[e], "hci", by(T.pkc[:, 96 * e:96 * e + 96]), by(T.hdc[:])) for e in cross])
+    wait("gq", [psc])
+    fused([(*hop[e], "hsi", T.pks[:, 96 * e:96 * e + 96], T.hds[:]) for e in cross])
+    at = lambda e: 48 * seat(e).index(me)
+    two = [(e, i, 96 * e + 48 * i, ("lxn", "lgn")[i]) for e in near for i in range(2)]
+    wait("gq", [nc])
+    fused([(cores[e], half(nhop[e], i), "nco", by(T.pkc[:, p:p + 48]), by(T[b + "c"][:, at(e):at(e) + 48])) for e, i, p, b in two])
+    wait("gq", [nsc])
+    fused([(cores[e], half(nhop[e], i), "nsc", T.pks[:, p:p + 48], T[b + "s"][:, at(e):at(e) + 48]) for e, i, p, b in two])
+    gid = G([vone], g.affine_select, C("idn"), C("ones"), [[-1, 128]], OP.is_equal, 0.0, 0, 1)
+
+    qw = quant([lw], "ww", 0, 512, T.win[:])
+    ve = V([], "set", T.e4[:], 0.0)
+    vk = V([], "set", T.kt[:], 0.0)
+    vl0 = V([], "set", C("la"), 0)
+    vset = None
+    for b in "nc":
+        V([], "set", T["big" + b][:, 2304:2816], 0.0)
+        vset = V([], "set", T["f" + b][:, 48:64], -1.0)
+    ie = None
+    for i in range(4):
+        ie = V([ve, gid], "copy", T.e4[:, 512 * i + i:512 * i + 512:4], C("idn"))
+    qe = quant([ie], "ee", 0, 512, T.e4[:])
+    qpr = quant([lpr], "pp", 0, 128, T.prin[:])
+    pp, pps = pickq([qpr, vl0], qp("pq"), qp("pp"), C("la"))
+    k1 = V([gip], "ts", C("ka"), C("ip"), 31, None, OP.bitwise_and)
+    k2 = V([k1], "ts", C("kb"), C("ka"), 15, None, OP.bitwise_and)
+    kc = V([k1], "copy", C("kcol", 0, 1), C("ka", 0, 1))
+    kc2 = V([k1], "ts", C("kcol", 1, 2), C("ka", 0, 1), 32, None, OP.add)
+    w0 = V([kc, gk48], "ts", C("wn", 0, 48), C("kx"), C("kcol", 0, 1), 2.0, OP.is_lt, OP.mult)
+    w1 = V([kc2, gk48], "ts", C("wn", 48, 96), C("kx"), C("kcol", 1, 2), 2.0, OP.is_lt, OP.mult)
+    wm = V([w0, w1], "ts", C("wm"), C("wn"), -1.0, None, OP.add)
+    lo = V([k2], "copy", C("kdol", 0, 2), C("kb", 0, 2))
+    hi = V([k1, k2], "tt", C("kdol", 2, 3), C("ka", 0, 1), C("kb", 0, 1), OP.subtract)
+    hi2 = V([], "set", C("kdol", 3, 4), 32.0)
+    kd, kl = VIEW["kdol"][1], None
+    for a in range(4):
+        p = slice(32 * a, 32 * a + 32)
+        lov, hiv, c = T.kf[p, kd:kd + 2], T.kf[p, kd + 2:kd + 4], 4 * a
+        V([lo, vk], "copy", T.kt[p, c:c + 2], lov)
+        V([lo, vk], "copy", T.kt[p, 16 + c:18 + c], lov)
+        V([hi, hi2, vk], "ts", T.kt[p, 512 + c:514 + c], hiv, 48.0 * a, None, OP.add)
+        kl = V([hi, hi2, vk], "copy", T.kt[p, 528 + c:530 + c], hiv)
+    qk = quant([kl], "kk", 0, 256, T.kt[:])
+    qu = quant([lu], "uu", 0, 512, T.ubin[:])
+
+    def expert(b, arrived):
+        B, F, M0, D0, H0 = T["big" + b], T["f" + b], 768, 1536, 2304
+        po, ll = T["po" + b], T["ll" + b]
+        fw, dd, mk, mt, dx = {}, {}, {}, {}, {}
+        for kind, i in (("f", 2), ("f", 0), ("d", 0), ("f", 3), ("f", 1), ("d", 1), ("d", 2), ("d", 3)):
+            l, r, o = ("ww", "lx" + b, i) if kind == "f" else ("ee", "lg" + b, 4 + i)
+            t = MM(arrived + [qw, qe] + used[o], PS[o][:, 0:192], qp(l, 128 * i, 128 * i + 128), qp(r), True, True)
+            (fw if kind == "f" else dd)[i] = t
+        mask = lambda i: B[:, 192 * i:192 * i + 192]
+        sgn = lambda i: B[:, D0 + 192 * i:D0 + 192 * i + 192]
+        for i in (2, 3):
+            used[i] = [S([fw[i]], sgn(i), PS[i][:, 0:192], AF.Sign)]
+            mk[i] = S(used[i], mask(i), sgn(i), AF.Relu)
+        for i in (0, 1):
+            mk[i] = V([fw[i]], "ts", mask(i), PS[i][:, 0:192], 0.0, None, OP.is_gt)
+            used[i] = [mk[i]]
+        for i in range(4):
+            mt[i] = V([mk[i], dd[i]], "tt", B[:, M0 + i:M0 + 768:4], PS[4 + i][:, 0:192], mask(i), OP.mult)
+            used[4 + i] = [mt[i]]
+        mts, mks = list(mt.values()), list(mk.values())
+        qm = quant(mts, "mm" + b, 0, 192, B[:, M0:M0 + 768])
+        st = MM([qm, pp, pps] + used[0], PS[0][:, 0:192], qp("pq"), qp("mm" + b), True, True)
+        um = [MM([qm, qu] + used[i + 1], PS[i + 1][:, 0:192], qp("uu", 128 * i, 128 * i + 128), qp("mm" + b), True, True) for i in range(4)]
+        ab = [S([st, vset], F[32 * a:32 * a + 32, 0:48], PS[0][32 * a:32 * a + 32, 48 * a:48 * a + 48], AF.Abs) for a in range(4)]
+        used[0] = ab[-1:]
+        tn = V(ab, "tr", F[:, 64:128], F[:, 0:64])
+        sg = [S([tn], F[:, 256 + 48 * t:304 + 48 * t], F[:, 0:48], AF.Sign, bias=F[:, 64 + 32 * t:65 + 32 * t], scale=-1.0, accum_out=F[:, 160 + t:161 + t]) for t in range(2)]
+        for i in range(4):
+            dx[i] = S([um[i]] + mks, B[:, D0 + i:D0 + 768:4], PS[i + 1][:, 0:192], AF.Copy, scale=0.0625)
+            used[i + 1] = [dx[i]]
+        eq = [V([tn] + mts, "ts", B[:, 48 * t:48 * t + 48], F[:, 0:48], F[:, 64 + 32 * t:65 + 32 * t], None, OP.is_equal) for t in range(2)]
+        em = V(eq + mts + [wm], "tt", B[:, 96:192], B[:, 0:96], C("wm"), OP.mult)
+        er = [V([em], "red", F[:, 176 + t:177 + t], B[:, 96 + 48 * t:144 + 48 * t], AX.X, OP.add) for t in range(2)]
+        rk = V(er + sg, "tt", F[:, 192:194], F[:, 176:178], F[:, 160:162], OP.subtract)
+        oh = [V([rk, gi2, vset], "ts", B[:, H0 + t:H0 + 512:4], C("its"), F[:, 192 + t:193 + t], None, OP.is_equal) for t in range(2)]
+        qo = quant(oh, "oh" + b, 0, 128, B[:, H0:H0 + 512])
+        MM([qo, qk] + used[5], PS[5][:, 0:128], qp("oh" + b), qp("kk", 0, 128), True, False)
+        lm = MM([qo, qk], PS[5][:, 0:128], qp("oh" + b), qp("kk", 128, 256), False, True)
+        vpo = V([lm], "copy", po[:], PS[5][:, 0:4])
+        vll = V([lm], "ts", ll[:], PS[5][:, 4:8], 64.0 * me, None, OP.add)
+        used[5] = [vpo, vll]
+        qd = quant(list(dx.values()), "dd" + b, 0, 192, B[:, D0:D0 + 768])
+        rc, rs = pickq([qd, vpo], qp("rr" + b), qp("dd" + b), po[:])
+        return qd, vpo, vll, rc, rs
+
+    qdn, pon, lln, rcn, rsn = expert("n", [("nco", 16), ("nsc", 16), ("selfcp", 64)])
+    back = lambda e: 64 + 16 * near_of(e).index(me)
+    ls = lambda e: seat(me).index(e)
+    wait("gq", [lln])
+    fused([(cores[e], nhop[e], "rln", T.lln[:, ls(e):ls(e) + 1], T.lland[:, 4 + near_of(e).index(me):5 + near_of(e).index(me)]) for e in near])
+    wait("gq", [rcn])
+    fused([(cores[e], nhop[e], "rcn", by(T.rrnc[:, 16 * ls(e):16 * ls(e) + 16]), by(T.camc[:, back(e):back(e) + 16])) for e in near])
+    wait("gq", [rsn])
+    fused([(cores[e], nhop[e], "rsn", T.rrns[:, 16 * ls(e):16 * ls(e) + 16], T.cams[:, back(e):back(e) + 16]) for e in near])
+    qzc = quant([vz], "cam", 128, 256, T.zt[:])
+    own, owns = pickq([qdn, pon], qp("cam", 112, 128), qp("ddn"), T.pon[:, 2:3])
+
+    ct = V([cum], "tr", C("ctr"), C("cum"))
+    va = V([ct], "ts", C("va"), C("ctr", 0, 128, 4), 49.0, None, OP.min)
+    vb = V([va, gcs], "tt", C("vb"), C("va"), C("cse"), OP.add)
+    ia = V([npn], "ts", C("iab", 0, 32), C("np"), 0.0, None, OP.is_equal)
+    ib = V([npn], "ts", C("iab", 32, 64), C("np"), 1.0, None, OP.is_equal)
+    ma = V([vb, ia], "tt", C("vab", 0, 32), C("vb"), C("iab", 0, 32), OP.mult)
+    mb = V([vb, ib], "tt", C("vab", 32, 64), C("vb"), C("iab", 32, 64), OP.mult)
+    h1 = V([ma, mb], "tt", C("vac"), C("vab", 0, 64, 2), C("vab", 1, 64, 2), OP.add)
+    h2 = V([h1], "tt", C("vad"), C("vac", 0, 32, 2), C("vac", 1, 32, 2), OP.add)
+    h3 = V([h2], "tt", C("vae"), C("vad", 0, 16, 2), C("vad", 1, 16, 2), OP.add)
+    og1 = V([h3], "copy", T.offg[:, 0:16:2], C("vae"))
+    og2 = V([h3], "copy", T.offg[:, 1:16:2], C("vae"))
+    vrs = V([], "set", T.rsw[:], 128.0)
+    vcf = V([], "set", C("cf"), 0.0)
+    qv = quant([lv], "vv", 0, 128, T.vin[:])
+
+    qdc, poc, llc, rcc, rsc = expert("c", [("cco", 32), ("csc", 32)])
+    wait("gq", [llc])
+    fused([(*hop[e], "hli", T.llc[:, i:i + 1], T.hrl[:, 0:1]) for i, e in enumerate(cross)])
+    wait("gq", [rcc])
+    fused([(*hop[e], "hri", by(T.rrcc[:, 16 * i:16 * i + 16]), by(T.hrc[:])) for i, e in enumerate(cross)])
+    wait("gq", [rsc])
+    fused([(*hop[e], "hrsi", T.rrcs[:, 16 * i:16 * i + 16], T.hrs[:]) for i, e in enumerate(cross)])
+
+    sc1 = V([vrs, lln, gva], "copy", T.rsw[:].indirect(T.lln[:, 2:3]), C("vals", 112, 128))
+    sc2 = V([sc1, ("rln", 16)], "copy", T.rsw[:].indirect(T.lland[:, 4:7]), C("vals", 64, 112))
+    sc3 = V([sc2, ("rlc", 32)], "copy", T.rsw[:].indirect(T.lland[:, 0:4]), C("vals", 0, 64))
+    gg = V([sc3, og1, og2], "copy", T.gg[:], T.rsw[:].indirect(T.offg[:]))
+    gt = V([gg], "tr", T.gt[:], T.gg[:])
+    fo = V([gt], "copy", T.fo[:], T.gt[:, 0:256:16])
+    f1 = V([gt], "ts", C("cfa"), T.gt[:, 0:128:16], 127.5, None, OP.is_lt)
+    f2 = V([gt], "ts", C("cfb"), T.gt[:, 128:256:16], 127.5, 2.0, OP.is_lt, OP.mult)
+    f3 = V([f1, f2, vcf], "tt", C("cf", 0, 8), C("cfa"), C("cfb"), OP.add)
+    f4 = V([f3], "tr", C("cft"), C("cf"))
+    wait("sync", [f4])
+    hf, o = VIEW["cft"][:2]
+    g.sync.dma_start(T.ct[:], T[hf][0:8, o:o + 16]).then_inc(T.sem.outs, 16)
+    arr = [("rcn", 16), ("rsn", 16), ("rcc", 32), ("rsc", 32), qzc, own, owns, fo]
+    zp, zs = pickq(arr, qp("zp"), qp("cam"), T.fo[:])
+    zt = []
+    for i in range(4):
+        l, o = qp("ee", 128 * i, 128 * i + 128), PS[i][:, 0:128]
+        MM([zp, zs] + used[i], o, l, qp("zp", 0, 128), True, False)
+        t = MM([], o, l, qp("zp", 128, 256), False, True)
+        zt.append(V([t], "copy", T.zz[:, i:512:4], o) if i % 2 else S([t], T.zz[:, i:512:4], o, AF.Copy))
+    zq = quant(zt, "zq", 0, 128, T.zz[:])
+    wait("sync", [zq])
+    wait("sq", [zq])
+    g.sync.dma_start(T.oc[:], by(T.zqc[:])).then_inc(T.sem.outs, 16)
+    for k in range(4):
+        (g.sync if k < 2 else g.scalar).dma_start(T.osc[4 * k:4 * k + 4, :], T.zqs[32 * k:32 * k + 4, :]).then_inc(T.sem["outs" if k < 2 else "outs2"], 16)
+    ym = MM([zq, qv] + used[4], PS[4][:, 0:128], qp("vv"), qp("zq"), True, True)
+    yc = V([ym], "copy", T.yo[:], PS[4][:, 0:128])
+    wait("sync", [yc])
+    g.sync.dma_start(T.y[:], T.yo[:]).then_inc(T.sem.outs, 16)
+
+    for s in ("vq", "sq", "tq", "gq"):
+        wait("gq", [(s, cnt[s])])
+    wait("gq", [lx, lrt, lgr, lw, lpr, lu, lv, ("outs", 80), ("outs2", 32), ("loc", loc[0])])

@@ -10,7 +10,7 @@ NS = 8
 F8, U8, U16, BF, F32, I32 = "float8_e4m3fn_x4", "uint8", "uint16", "bfloat16", "float32", "int32"
 SCRATCH = {}
 for _n, _w in dict(xin=512, grin=512, rtin=512, win=2048, ubin=2048, prin=512, vin=512, zt=512, e4=2048, kt=1024,
-                   cb=2048, jk=2048, rsw=512, gg=256, gt=256, zz=512, bign=2816, bigc=2816).items():
+                   cb=2048, jk=2048, rsw=512, gg=256, gt=256, zz=512, bign=3008, bigc=3008).items():
     SCRATCH[_n] = ("sbuf", [128, _w], BF)
 for _n, _w in dict(own=512, rt=128, rp=128, ww=512, uu=512, pp=128, pq=128, vv=128, ee=512, kk=256, pk=768, hd=96, hr=16, cam=256,
                    zp=256, zq=128, lxn=192, lgn=192, mmn=192, ddn=192, ohn=128, rrn=64, lxc=192, lgc=192, mmc=192, ddc=192, ohc=128, rrc=64).items():
@@ -86,10 +86,10 @@ def hand_on(g, core, T, topo):
     def two(sem, srcs, dsts):
         g.remote_dma_fused([RemoteDMATransfer(dst_ids=[DstId(rid=rid, pnc=pid)], dma_engine_mask=m, remote_sem=T.sem[sem], src=s, dst=d)
                             for m, s, d in zip(hs, srcs, dsts)], local_sem=T.sem.loc)
-    g.wait_ge(T.sem.hci, 4)
-    two("cco", [by(T.hdc[:, 0:48]), by(T.hdc[:, 48:96])], [by(T.lxcc[:, a:a + 48]), by(T.lgcc[:, a:a + 48])])
     g.wait_ge(T.sem.hsi, 4)
     two("csc", [T.hds[:, 0:48], T.hds[:, 48:96]], [T.lxcs[:, a:a + 48], T.lgcs[:, a:a + 48]])
+    g.wait_ge(T.sem.hci, 4)
+    two("cco", [by(T.hdc[:, 0:48]), by(T.hdc[:, 48:96])], [by(T.lxcc[:, a:a + 48]), by(T.lgcc[:, a:a + 48])])
     a = 16 * k
     for sem, rsem, src, to in (("hli", "rlc", T.hrl[:, 0:1], T.lland[:, k:k + 1]),
                                ("hri", "rcc", by(T.hrc[:]), by(T.camc[:, a:a + 16])),
@@ -287,10 +287,10 @@ def rank_program(g, core, T, topo):
             nhop[e], kb = offe[kb:kb + 4], kb + 4
     half = lambda l, i: l[len(l) // 2 * i:len(l) // 2 * (i + 1)]
 
-    wait("gq", [pc])
-    fused([(*hop[e], "hci", by(T.pkc[:, 96 * e:96 * e + 96]), by(T.hdc[:])) for e in cross])
     wait("gq", [psc])
     fused([(*hop[e], "hsi", T.pks[:, 96 * e:96 * e + 96], T.hds[:]) for e in cross])
+    wait("gq", [pc])
+    fused([(*hop[e], "hci", by(T.pkc[:, 96 * e:96 * e + 96]), by(T.hdc[:])) for e in cross])
     at = lambda e: 48 * seat(e).index(me)
     two = [(e, i, 96 * e + 48 * i, ("lxn", "lgn")[i]) for e in near for i in range(2)]
     wait("gq", [nc])
@@ -334,63 +334,6 @@ def rank_program(g, core, T, topo):
     qk = quant([kl], "kk", 0, 256, T.kt[:])
     qu = quant([lu], "uu", 0, 512, T.ubin[:])
 
-    def expert(b, arrived):
-        B, F, M0, D0, H0 = T["big" + b], T["f" + b], 768, 1536, 2304
-        po, ll = T["po" + b], T["ll" + b]
-        fw, dd, mk, mt, dx = {}, {}, {}, {}, {}
-        for kind, i in (("f", 2), ("f", 0), ("d", 0), ("f", 3), ("f", 1), ("d", 1), ("d", 2), ("d", 3)):
-            l, r, o = ("ww", "lx" + b, i) if kind == "f" else ("ee", "lg" + b, 4 + i)
-            t = MM(arrived + [qw, qe] + used[o], PS[o][:, 0:192], qp(l, 128 * i, 128 * i + 128), qp(r), True, True)
-            (fw if kind == "f" else dd)[i] = t
-        mask = lambda i: B[:, 192 * i:192 * i + 192]
-        sgn = lambda i: B[:, D0 + 192 * i:D0 + 192 * i + 192]
-        for i in (2, 3):
-            used[i] = [S([fw[i]], sgn(i), PS[i][:, 0:192], AF.Sign)]
-            mk[i] = S(used[i], mask(i), sgn(i), AF.Relu)
-        for i in (0, 1):
-            mk[i] = V([fw[i]], "ts", mask(i), PS[i][:, 0:192], 0.0, None, OP.is_gt)
-            used[i] = [mk[i]]
-        for i in range(4):
-            mt[i] = V([mk[i], dd[i]], "tt", B[:, M0 + i:M0 + 768:4], PS[4 + i][:, 0:192], mask(i), OP.mult)
-            used[4 + i] = [mt[i]]
-        mts, mks = list(mt.values()), list(mk.values())
-        qm = quant(mts, "mm" + b, 0, 192, B[:, M0:M0 + 768])
-        st = MM([qm, pp, pps] + used[0], PS[0][:, 0:192], qp("pq"), qp("mm" + b), True, True)
-        um = [MM([qm, qu] + used[i + 1], PS[i + 1][:, 0:192], qp("uu", 128 * i, 128 * i + 128), qp("mm" + b), True, True) for i in range(4)]
-        ab = [S([st, vset], F[32 * a:32 * a + 32, 0:48], PS[0][32 * a:32 * a + 32, 48 * a:48 * a + 48], AF.Abs) for a in range(4)]
-        used[0] = ab[-1:]
-        tn = V(ab, "tr", F[:, 64:128], F[:, 0:64])
-        sg = [S([tn], F[:, 256 + 48 * t:304 + 48 * t], F[:, 0:48], AF.Sign, bias=F[:, 64 + 32 * t:65 + 32 * t], scale=-1.0, accum_out=F[:, 160 + t:161 + t]) for t in range(2)]
-        for i in range(4):
-            dx[i] = S([um[i]] + mks, B[:, D0 + i:D0 + 768:4], PS[i + 1][:, 0:192], AF.Copy, scale=0.0625)
-            used[i + 1] = [dx[i]]
-        eq = [V([tn] + mts, "ts", B[:, 48 * t:48 * t + 48], F[:, 0:48], F[:, 64 + 32 * t:65 + 32 * t], None, OP.is_equal) for t in range(2)]
-        em = V(eq + mts + [wm], "tt", B[:, 96:192], B[:, 0:96], C("wm"), OP.mult)
-        er = [V([em], "red", F[:, 176 + t:177 + t], B[:, 96 + 48 * t:144 + 48 * t], AX.X, OP.add) for t in range(2)]
-        rk = V(er + sg, "tt", F[:, 192:194], F[:, 176:178], F[:, 160:162], OP.subtract)
-        oh = [V([rk, gi2, vset], "ts", B[:, H0 + t:H0 + 512:4], C("its"), F[:, 192 + t:193 + t], None, OP.is_equal) for t in range(2)]
-        qo = quant(oh, "oh" + b, 0, 128, B[:, H0:H0 + 512])
-        MM([qo, qk] + used[5], PS[5][:, 0:128], qp("oh" + b), qp("kk", 0, 128), True, False)
-        lm = MM([qo, qk], PS[5][:, 0:128], qp("oh" + b), qp("kk", 128, 256), False, True)
-        vpo = V([lm], "copy", po[:], PS[5][:, 0:4])
-        vll = V([lm], "ts", ll[:], PS[5][:, 4:8], 64.0 * me, None, OP.add)
-        used[5] = [vpo, vll]
-        qd = quant(list(dx.values()), "dd" + b, 0, 192, B[:, D0:D0 + 768])
-        rc, rs = pickq([qd, vpo], qp("rr" + b), qp("dd" + b), po[:])
-        return qd, vpo, vll, rc, rs
-
-    qdn, pon, lln, rcn, rsn = expert("n", [("nco", 16), ("nsc", 16), ("selfcp", 64)])
-    back = lambda e: 64 + 16 * near_of(e).index(me)
-    ls = lambda e: seat(me).index(e)
-    wait("gq", [lln])
-    fused([(cores[e], nhop[e], "rln", T.lln[:, ls(e):ls(e) + 1], T.lland[:, 4 + near_of(e).index(me):5 + near_of(e).index(me)]) for e in near])
-    wait("gq", [rcn])
-    fused([(cores[e], nhop[e], "rcn", by(T.rrnc[:, 16 * ls(e):16 * ls(e) + 16]), by(T.camc[:, back(e):back(e) + 16])) for e in near])
-    wait("gq", [rsn])
-    fused([(cores[e], nhop[e], "rsn", T.rrns[:, 16 * ls(e):16 * ls(e) + 16], T.cams[:, back(e):back(e) + 16]) for e in near])
-    qzc = quant([vz], "cam", 128, 256, T.zt[:])
-    own, owns = pickq([qdn, pon], qp("cam", 112, 128), qp("ddn"), T.pon[:, 2:3])
-
     ct = V([cum], "tr", C("ctr"), C("cum"))
     va = V([ct], "ts", C("va"), C("ctr", 0, 128, 4), 49.0, None, OP.min)
     vb = V([va, gcs], "tt", C("vb"), C("va"), C("cse"), OP.add)
@@ -406,8 +349,79 @@ def rank_program(g, core, T, topo):
     vrs = V([], "set", T.rsw[:], 128.0)
     vcf = V([], "set", C("cf"), 0.0)
     qv = quant([lv], "vv", 0, 128, T.vin[:])
+    qzc = quant([vz], "cam", 128, 256, T.zt[:])
 
-    qdc, poc, llc, rcc, rsc = expert("c", [("cco", 32), ("csc", 32)])
+    R, QUARTERS = {}, range(4)
+    come = {"n": [("nco", 16), ("nsc", 16), ("selfcp", 64)], "c": [("cco", 32), ("csc", 32)]}
+    dbank = {"c": (4, 5, 6, 7), "n": (1, 2, 3, 4)}
+
+    def products(b, todo):
+        for kind, i in todo:
+            l, r, o = ("ww", "lx" + b, i) if kind == "f" else ("ee", "lg" + b, dbank[b][i])
+            R[b, kind, i] = MM(come[b] + [qw, qe] + used[o], PS[o][:, 0:192], qp(l, 128 * i, 128 * i + 128), qp(r), True, True)
+
+    def mask_s(b, i):
+        B = T["big" + b]
+        m = B[:, 1536 + 192 * i:1728 + 192 * i]
+        used[i] = [S([R[b, "f", i]], m, PS[i][:, 0:192], AF.Sign)]
+        R[b, "k", i] = S(used[i], B[:, 192 * i:192 * i + 192], m, AF.Relu)
+
+    def mask_v(b, i):
+        R[b, "k", i] = V([R[b, "f", i]], "ts", T["big" + b][:, 192 * i:192 * i + 192], PS[i][:, 0:192], 0.0, None, OP.is_gt)
+        used[i] = [R[b, "k", i]]
+
+    def masked(b, i):
+        B, o = T["big" + b], dbank[b][i]
+        R[b, "m", i] = V([R[b, "k", i], R[b, "d", i]], "tt", B[:, 768 + i:1536:4], PS[o][:, 0:192], B[:, 192 * i:192 * i + 192], OP.mult)
+        used[o] = [R[b, "m", i]]
+
+    def strengths(b, sbank, ubank, between):
+        B, F = T["big" + b], T["f" + b]
+        qm = quant([R[b, "m", i] for i in QUARTERS], "mm" + b, 0, 192, B[:, 768:1536])
+        st = MM([qm, pp, pps] + used[sbank], PS[sbank][:, 0:192], qp("pq"), qp("mm" + b), True, True)
+        between()
+        um = [MM([qm, qu] + used[ubank[i]], PS[ubank[i]][:, 0:192], qp("uu", 128 * i, 128 * i + 128), qp("mm" + b), True, True) for i in QUARTERS]
+        ab = [S([st, vset], F[32 * a:32 * a + 32, 0:48], PS[sbank][32 * a:32 * a + 32, 48 * a:48 * a + 48], AF.Abs) for a in range(4)]
+        used[sbank] = ab[-1:]
+        tn = V(ab, "tr", F[:, 64:128], F[:, 0:64])
+
+        def scaled(i):
+            R[b, "x", i] = S([um[i]] + [R[b, "k", j] for j in QUARTERS], B[:, 1536 + i:2304:4], PS[ubank[i]][:, 0:192], AF.Copy, scale=0.0625)
+            used[ubank[i]] = [R[b, "x", i]]
+        scaled(0)
+        sg = [S([tn], F[:, 256 + 48 * t:304 + 48 * t], F[:, 0:48], AF.Sign, bias=F[:, 64 + 32 * t:65 + 32 * t], scale=-1.0, accum_out=F[:, 160 + t:161 + t]) for t in range(2)]
+        for i in (1, 2, 3):
+            scaled(i)
+        eq = [V([tn], "ts", B[:, 2816 + 48 * t:2864 + 48 * t], F[:, 0:48], F[:, 64 + 32 * t:65 + 32 * t], None, OP.is_equal) for t in range(2)]
+        em = V(eq + [wm], "tt", B[:, 2912:3008], B[:, 2816:2912], C("wm"), OP.mult)
+        er = [V([em], "red", F[:, 176 + t:177 + t], B[:, 2912 + 48 * t:2960 + 48 * t], AX.X, OP.add) for t in range(2)]
+        rk = V(er + sg, "tt", F[:, 192:194], F[:, 176:178], F[:, 160:162], OP.subtract)
+        oh = [V([rk, gi2, vset], "ts", B[:, 2304 + t:2816:4], C("its"), F[:, 192 + t:193 + t], None, OP.is_equal) for t in range(2)]
+        R[b, "q"] = quant(oh, "oh" + b, 0, 128, B[:, 2304:2816])
+
+    def answers(b, o, between):
+        po, ll = T["po" + b], T["ll" + b]
+        MM([R[b, "q"], qk] + used[o], PS[o][:, 0:128], qp("oh" + b), qp("kk", 0, 128), True, False)
+        lm = MM([], PS[o][:, 0:128], qp("oh" + b), qp("kk", 128, 256), False, True)
+        between()
+        vll = V([lm], "ts", ll[:], PS[o][:, 4:8], 64.0 * me, None, OP.add)
+        vpo = V([lm], "copy", po[:], PS[o][:, 0:4])
+        used[o] = [vpo, vll]
+        qd = quant([R[b, "x", i] for i in QUARTERS], "dd" + b, 0, 192, T["big" + b][:, 1536:2304])
+        rc, rs = pickq([qd, vpo], qp("rr" + b), qp("dd" + b), po[:])
+        return qd, vpo, vll, rc, rs
+
+    products("c", (("f", 0), ("f", 2), ("d", 0), ("f", 1), ("d", 1), ("f", 3), ("d", 2), ("d", 3)))
+    for i in (2, 3):
+        mask_s("c", i)
+    for i in QUARTERS:
+        if i < 2:
+            mask_v("c", i)
+        masked("c", i)
+    products("n", [("f", i) for i in QUARTERS])
+    strengths("c", 4, (5, 6, 7, 0), lambda: [mask_v("n", i) for i in QUARTERS])
+    products("n", [("d", i) for i in QUARTERS])
+    qdc, poc, llc, rcc, rsc = answers("c", 5, lambda: [masked("n", i) for i in (0, 1)])
     wait("gq", [llc])
     fused([(*hop[e], "hli", T.llc[:, i:i + 1], T.hrl[:, 0:1]) for i, e in enumerate(cross)])
     wait("gq", [rcc])
@@ -415,12 +429,28 @@ def rank_program(g, core, T, topo):
     wait("gq", [rsc])
     fused([(*hop[e], "hrsi", T.rrcs[:, 16 * i:16 * i + 16], T.hrs[:]) for i, e in enumerate(cross)])
 
+    for i in (2, 3):
+        masked("n", i)
+    strengths("n", 6, (7, 0, 1, 2), lambda: None)
+    qdn, pon, lln, rcn, rsn = answers("n", 3, lambda: None)
+    back = lambda e: 64 + 16 * near_of(e).index(me)
+    ls = lambda e: seat(me).index(e)
+    wait("gq", [lln])
+    fused([(cores[e], nhop[e], "rln", T.lln[:, ls(e):ls(e) + 1], T.lland[:, 4 + near_of(e).index(me):5 + near_of(e).index(me)]) for e in near])
+    wait("gq", [rcn])
+    fused([(cores[e], nhop[e], "rcn", by(T.rrnc[:, 16 * ls(e):16 * ls(e) + 16]), by(T.camc[:, back(e):back(e) + 16])) for e in near])
+    wait("gq", [rsn])
+    fused([(cores[e], nhop[e], "rsn", T.rrns[:, 16 * ls(e):16 * ls(e) + 16], T.cams[:, back(e):back(e) + 16]) for e in near])
+    own, owns = pickq([qdn, pon], qp("cam", 112, 128), qp("ddn"), T.pon[:, 2:3])
+
     sc1 = V([vrs, lln, gva], "copy", T.rsw[:].indirect(T.lln[:, 2:3]), C("vals", 112, 128))
     sc2 = V([sc1, ("rln", 16)], "copy", T.rsw[:].indirect(T.lland[:, 4:7]), C("vals", 64, 112))
     sc3 = V([sc2, ("rlc", 32)], "copy", T.rsw[:].indirect(T.lland[:, 0:4]), C("vals", 0, 64))
     gg = V([sc3, og1, og2], "copy", T.gg[:], T.rsw[:].indirect(T.offg[:]))
     gt = V([gg], "tr", T.gt[:], T.gg[:])
     fo = V([gt], "copy", T.fo[:], T.gt[:, 0:256:16])
+    arr = [("rcn", 16), ("rsn", 16), ("rcc", 32), ("rsc", 32), qzc, own, owns, fo]
+    zp, zs = pickq(arr, qp("zp"), qp("cam"), T.fo[:])
     f1 = V([gt], "ts", C("cfa"), T.gt[:, 0:128:16], 127.5, None, OP.is_lt)
     f2 = V([gt], "ts", C("cfb"), T.gt[:, 128:256:16], 127.5, 2.0, OP.is_lt, OP.mult)
     f3 = V([f1, f2, vcf], "tt", C("cf", 0, 8), C("cfa"), C("cfb"), OP.add)
@@ -428,10 +458,8 @@ def rank_program(g, core, T, topo):
     wait("sync", [f4])
     hf, o = VIEW["cft"][:2]
     g.sync.dma_start(T.ct[:], T[hf][0:8, o:o + 16]).then_inc(T.sem.outs, 16)
-    arr = [("rcn", 16), ("rsn", 16), ("rcc", 32), ("rsc", 32), qzc, own, owns, fo]
-    zp, zs = pickq(arr, qp("zp"), qp("cam"), T.fo[:])
     zt = []
-    for i in range(4):
+    for i in QUARTERS:
         l, o = qp("ee", 128 * i, 128 * i + 128), PS[i][:, 0:128]
         MM([zp, zs] + used[i], o, l, qp("zp", 0, 128), True, False)
         t = MM([], o, l, qp("zp", 128, 256), False, True)

@@ -5,14 +5,16 @@ OP, AX, AF = AluOpType, AxisListType, ActivationFunctionType
 N, CAPP, CAPR = 8, 48, 16
 SIM = 256
 BIG = 9.0e29
-NS = 8
+NS = 7
+NV = 16 - NS
+OWN = 130
 
 F8, U8, U16, BF, F32, I32 = "float8_e4m3fn_x4", "uint8", "uint16", "bfloat16", "float32", "int32"
 SCRATCH = {}
-for _n, _w in dict(xin=512, grin=512, rtin=512, win=2048, ubin=2048, prin=512, vin=512, zt=512, e4=2048, kt=1024,
-                   cb=2048, jk=2048, rsw=512, gg=256, gt=256, zz=512, bign=3008, bigc=3008).items():
+for _n, _w in dict(xin=4 * OWN, grin=4 * OWN, rtin=512, win=2048, ubin=2048, prin=512, vin=512, zt=512, e4=2048, kt=544,
+                   cb=128 * NV, cn=128 * NV, rm=128 * NV, jk=2048, rsw=512, gg=256, gt=256, zz=512, bign=2912, bigc=2912).items():
     SCRATCH[_n] = ("sbuf", [128, _w], BF)
-for _n, _w in dict(own=512, rt=128, rp=128, ww=512, uu=512, pp=128, pq=128, vv=128, ee=512, kk=256, pk=768, hd=96, hr=16, cam=256,
+for _n, _w in dict(own=2 * OWN, rt=128, rp=128, ww=512, uu=512, pp=128, pq=128, vv=128, ee=512, kk=136, pk=768, hd=96, hr=16, cam=256,
                    zp=256, zq=128, lxn=192, lgn=192, mmn=192, ddn=192, ohn=128, rrn=64, lxc=192, lgc=192, mmc=192, ddc=192, ohc=128, rrc=64).items():
     SCRATCH[_n + "c"] = ("sbuf", [128, _w], F8)
     SCRATCH[_n + "s"] = ("sbuf", [128, _w], U8)
@@ -23,9 +25,9 @@ for _n, _w in dict(st=160, fn=512, fc=512, yo=128).items():
 for _i in range(8):
     SCRATCH["ps%d" % _i] = ("psum", [128, 512], F32)
 VIEW = {}
-for _b, _d, _l in (("ii", I32, "ip8 ic8 ra8 ta8 tb8 ua8 ub8 uc8 ud8 sa8 sb8 sc8 ka8 kb8 kq8 ea8 eb8 ec8 ed8 ef8"),
+for _b, _d, _l in (("ii", I32, "ip8 ic8 ra8 ta8 tb8 ua8 ub8 uc8 ud8 sa8 sb8 sc8 ka8 kb8 kq8 qi8 ci8 ea8 eb8 ec8 ed8 ef8"),
                    ("lu", U16, "la8 lb8 lc8 ld8"),
-                   ("kf", F32, "kcol8 kdol8 kthr8 kr16 kk16 nk16 kx48 cse32 rs32"),
+                   ("kf", F32, "kcol8 klo8 kh8 khx8 kix8 mk8 kthr8 kr16 kk16 nk16 kx48 cse32 rs32"),
                    ("kb", BF, "vals128 its128 idn128 ones128 wn96 wm96"),
                    ("df", F32, "xd32 xo32 va32 vb32 iab64 vab64 vac32 vad16 vae8 xa16 pfa32 pra32 pfb32 prb32 vf40 vr40"),
                    ("db", BF, "fb128 ft128 cum128 ctr128 nla32 nlb32 nra32 nrb32 nl32 nr32 np32"),
@@ -38,7 +40,7 @@ for _b, _d, _l in (("ii", I32, "ip8 ic8 ra8 ta8 tb8 ua8 ub8 uc8 ud8 sa8 sb8 sc8 
     SCRATCH[_b] = ("sbuf", [128, _o], _d)
 
 SEMAPHORES = ["vq", "sq", "tq", "gq", "ldx", "ldrt", "ldgr", "ldpr", "ldw", "ldu", "ldv", "selfcp", "outs", "outs2", "loc",
-              "hci", "hsi", "hli", "hri", "hrsi", "cco", "csc", "nco", "nsc", "rlc", "rcc", "rsc", "rln", "rcn", "rsn"]
+              "hci", "hsi", "hli", "hri", "hrsi", "cxo", "cgo", "csc", "nco", "nsc", "rlc", "rcc", "rsc", "rln", "rcn", "rsn"]
 
 
 def roads(T, topo):
@@ -82,21 +84,19 @@ def hand_on(g, core, T, topo):
     al, hs = bits(es), (bits(es[:len(es) // 2]), bits(es[len(es) // 2:]))
     k = cross[e].index(q)
     a = k * CAPP
-
-    def two(sem, srcs, dsts):
-        g.remote_dma_fused([RemoteDMATransfer(dst_ids=[DstId(rid=rid, pnc=pid)], dma_engine_mask=m, remote_sem=T.sem[sem], src=s, dst=d)
-                            for m, s, d in zip(hs, srcs, dsts)], local_sem=T.sem.loc)
     g.wait_ge(T.sem.hsi, 4)
-    two("csc", [T.hds[:, 0:48], T.hds[:, 48:96]], [T.lxcs[:, a:a + 48], T.lgcs[:, a:a + 48]])
-    g.wait_ge(T.sem.hci, 4)
-    two("cco", [by(T.hdc[:, 0:48]), by(T.hdc[:, 48:96])], [by(T.lxcc[:, a:a + 48]), by(T.lgcc[:, a:a + 48])])
-    a = 16 * k
-    for sem, rsem, src, to in (("hli", "rlc", T.hrl[:, 0:1], T.lland[:, k:k + 1]),
-                               ("hri", "rcc", by(T.hrc[:]), by(T.camc[:, a:a + 16])),
-                               ("hrsi", "rsc", T.hrs[:], T.cams[:, a:a + 16])):
-        g.wait_ge(T.sem[sem], 4)
+    g.remote_dma_fused([RemoteDMATransfer(dst_ids=[DstId(rid=rid, pnc=pid)], dma_engine_mask=m, remote_sem=T.sem.csc, src=s, dst=d)
+                        for m, s, d in ((hs[0], T.hds[:, 0:48], T.lxcs[:, a:a + 48]), (hs[1], T.hds[:, 48:96], T.lgcs[:, a:a + 48]))], local_sem=T.sem.loc)
+    b = 16 * k
+    for sem, rsem, src, to in (("hci", "cxo", by(T.hdc[:, 0:48]), by(T.lxcc[:, a:a + 48])),
+                               ("hci", "cgo", by(T.hdc[:, 48:96]), by(T.lgcc[:, a:a + 48])),
+                               ("hli", "rlc", T.hrl[:, 0:1], T.lland[:, k:k + 1]),
+                               ("hri", "rcc", by(T.hrc[:]), by(T.camc[:, b:b + 16])),
+                               ("hrsi", "rsc", T.hrs[:], T.cams[:, b:b + 16])):
+        if rsem != "cgo":
+            g.wait_ge(T.sem[sem], 4)
         g.remote_dma(to, src, T.sem[rsem], T.sem.loc, pid, rid, al)
-    g.wait_ge(T.sem.loc, 5 * len(es))
+    g.wait_ge(T.sem.loc, 6 * len(es))
 
 
 def rank_program(g, core, T, topo):
@@ -158,27 +158,36 @@ def rank_program(g, core, T, topo):
     def load(q, sem, out, in_):
         q.dma_start(out, in_).then_inc(T.sem[sem], 16)
         return (sem, 16)
-    lx = load(g.sync, "ldx", T.xin[:], T.x[:])
-    lrt = load(g.scalar, "ldrt", T.rtin[:], T.rt[:])
-    lgr = load(g.sync, "ldgr", T.grin[:], T.gr[:])
-    lw = load(g.scalar, "ldw", T.win[:], T.w[:])
-    lpr = load(g.sync, "ldpr", T.prin[:], T.pr[:])
+    lx = load(g.sync, "ldx", T.xin[:, 0:512], T.x[:])
+    lrt = load(g.scalar, "ldrt", T.rtin[:, 0:32], T.rt[:, 0:32])
+    lgr = load(g.sync, "ldgr", T.grin[:, 0:512], T.gr[:])
+    lpr = load(g.scalar, "ldpr", T.prin[:], T.pr[:])
+    lw = load(g.sync, "ldw", T.win[:], T.w[:])
     lu = load(g.sync, "ldu", T.ubin[:], T.ub[:])
     lv = load(g.scalar, "ldv", T.vin[:], T.v[:])
 
-    iota = lambda n, pat, base, cm: G([], g.iota, C(n), pat, base, cm, allow_small_or_imprecise_dtypes=True)
+    flags = dict(allow_small_or_imprecise_dtypes=True)
+    iota = lambda n, pat, base, cm: G([], g.iota, C(n), pat, base, cm, **flags)
     gip = G([], g.iota, C("ip"), [[0, 8]], 0, 1)
     gic = G([], g.iota, C("ic"), [[16, 8]], 0, 0)
     gkr = iota("kr", [[1, 16]], 0, 0)
+    gon = iota("ones", [[0, 128]], 1, 0)
+    gid = G([gon], g.affine_select, C("idn"), C("ones"), [[-1, 128]], OP.is_equal, 0.0, 0, 1)
+    grm = G([], g.iota, T.rm[:], [[0, 128 * NV]], 1, 0, **flags)
+    grm = G([grm], g.iota, T.rm[:, 0:128 * NV:128], [[0, NV]], 0, 0, **flags)
+    gva = iota("vals", [[1, 128]], 0, 0)
     gcs = iota("cse", [[0, 4], [64, 8]], -1, 0)
     gk48 = iota("kx", [[1, 48]], 0, 0)
-    gi2 = iota("its", [[0, 8], [2, 16]], -48, 0)
-    gva = iota("vals", [[1, 128]], 0, 0)
+    gi2 = iota("its", [[0, 8], [-2, 16]], 46, 0)
+    gci = G([], g.iota, C("ci"), [[0, 2], [1, 4]], 0, 0)
     vz = V([], "set", T.zt[:], 0.0)
-    vone = V([], "set", C("ones"), 1.0)
+    vxt = V([], "set", T.xin[:, 512:4 * OWN], 0.0)
     vr1 = V([], "set", C("rs"), BIG)
     vs1 = V([], "set", T.st[:, 0:32], 0.0)
     vs2 = [V([], "set", C(n, 0, 8), 0.0) for n in ("vf", "vr")][1]
+    fill = lambda out: S([vz], out, T.zt[:, 0:out.shape[1]], AF.Copy)
+    frt = fill(T.rtin[:, 32:512])
+    fe = [fill(T.e4[:, 0:512])]
     ra = V([gip], "ts", C("ra"), C("ip"), 15, None, OP.bitwise_and)
     vr2 = V([vr1], "set", C("rs", 0, 32, 8), -BIG)
     ua = V([ra], "ts", C("ua"), C("ra"), 7, None, OP.bitwise_and)
@@ -192,24 +201,24 @@ def rank_program(g, core, T, topo):
     sc = V([sa, sb], "tt", C("sc"), C("sa"), C("sb"), OP.add)
     ec = V([eb], "ts", C("ec"), C("eb"), -2, 7, OP.mult, OP.add)
     ed = V([ec, tb], "tt", C("ed"), C("ec"), C("tb"), OP.mult)
-    ef = V([ed], "tt", C("ef"), C("ed"), C("eb"), OP.add)
-    l1 = V([ef], "copy", C("lb"), C("ef"))
-    uc = V([ub], "tt", C("uc"), C("ub"), C("ra"), OP.add)
-    l3 = V([sc], "copy", C("ld"), C("sc"))
-    ud = V([uc], "tt", C("ud"), C("uc"), C("ic"), OP.add)
     kq = V([gip], "ts", C("kq"), C("ip"), 3, None, OP.bitwise_and)
-    l2 = V([ud], "copy", C("lc"), C("ud"))
+    ef = V([ed], "tt", C("ef"), C("ed"), C("eb"), OP.add)
+    uc = V([ub], "tt", C("uc"), C("ub"), C("ra"), OP.add)
+    l1 = V([ef], "copy", C("lb"), C("ef"))
+    ud = V([uc], "tt", C("ud"), C("uc"), C("ic"), OP.add)
     kt = V([kq], "ts", C("kthr"), C("kq"), 16, None, OP.mult)
+    l3 = V([sc], "copy", C("ld"), C("sc"))
+    l2 = V([ud], "copy", C("lc"), C("ud"))
     kk = V([kt, gkr], "ts", C("kk"), C("kr"), C("kthr", 0, 1), None, OP.add)
+    vgt = V([], "set", T.grin[:, 512:4 * OWN], 0.0)
     nk = V([kk], "ts", C("nk"), C("kk"), -1.0, -0.5, OP.mult, OP.add)
-    qz1 = quant([vz], "own", 128, 256, T.zt[:])
-    qz2 = quant([vz], "own", 384, 512, T.zt[:])
 
-    qrt = quant([lrt], "rt", 0, 128, T.rtin[:])
+    qrt = quant([lrt, frt], "rt", 0, 128, T.rtin[:])
     prt, prs = pickq([qrt, l1], qp("rp"), qp("rt"), C("lb"))
-    qx = quant([lx], "own", 0, 128, T.xin[:])
+    fe += [fill(T.e4[:, 512 * i:512 * i + 512]) for i in (1, 2, 3)]
+    qx = quant([lx, vxt], "own", 0, OWN, T.xin[:])
     ms = MM([prt, prs, qx], PS[0][:, 0:128], qp("rp"), qp("own", 0, 128), True, True)
-    qg = quant([lgr], "own", 256, 384, T.grin[:])
+    qg = quant([lgr, vgt], "own", OWN, 2 * OWN, T.grin[:])
     tr = V([ms, vs1], "tr", T.st[:, 32:160], PS[0][:, 0:128])
     used[0] = [tr]
     X = [T.st[:, 32 + u:160:4] for u in range(2)]
@@ -229,31 +238,36 @@ def rank_program(g, core, T, topo):
     sa = None
     for r in range(NS):
         sa = S([cum, nk], T.jk[:, 128 * r:128 * r + 128], C("cum"), AF.Sign, bias=C("nk", r, r + 1), accum_out=C("xa", r, r + 1))
-    cmps = [V([cum, kk], "ts", T.cb[:, 128 * r:128 * r + 128], C("cum"), C("kk", r, r + 1), None, OP.is_le) for r in range(NS, 16)]
-    red = None
+    d2, d3 = [S([sa], C("xd", h, h + NS), C("xa", 0, NS), AF.Copy, scale=-0.5, bias=64.0) for h in (0, 16)]
+    cm = None
     for r in range(NS, 16):
-        red = V([cmps[r - NS]], "red", C("xd", r, r + 1), T.cb[:, 128 * r:128 * r + 128], AX.X, OP.add)
-    d1 = V([red], "copy", C("xd", 16 + NS, 32), C("xd", NS, 16))
-    d2 = V([sa], "ts", C("xd", 0, NS), C("xa", 0, NS), -0.5, 64.0, OP.mult, OP.add)
-    d3 = V([sa], "ts", C("xd", 16, 16 + NS), C("xa", 0, NS), -0.5, 64.0, OP.mult, OP.add)
+        k = 128 * (r - NS)
+        cm = V([cum, kk], "ts", T.cb[:, k:k + 128], C("cum"), C("kk", r, r + 1), None, OP.is_le)
+    sn = V([cm, grm], "scan", T.cn[:], T.rm[:], T.cb[:], 0.0, OP.mult, OP.add)
+    d1 = [V([sn], "copy", C("xd", h + NS, h + 16), T.cn[:, 127:128 * NV:128]) for h in (0, 16)][1]
     xo = V([d1, d2, d3], "tr", C("xo"), C("xd"))
     of = None
     for c in range(3):
         V([xo], "copy", T.off[:, c:48:6], C("xo", c, 32, 4))
-        of = V([xo], "ts", T.off[:, 3 + c:48:6], C("xo", c, 32, 4), 256.0, None, OP.add)
+        of = V([xo], "ts", T.off[:, 3 + c:48:6], C("xo", c, 32, 4), float(OWN), None, OP.add)
 
-    def pick(es):
-        runs, r = [], None
+    def runs(es):
+        l = []
         for e in sorted(es):
-            if runs and runs[-1][1] == e:
-                runs[-1][1] = e + 1
+            if l and l[-1][1] == e:
+                l[-1][1] = e + 1
             else:
-                runs.append([e, e + 1])
-        for lo, hi in runs:
-            r = pickq([of, qz1, qz2, qx, qg], qp("pk", 96 * lo, 96 * hi), qp("own"), T.off[:, 6 * lo:6 * hi])
-        return r
-    pc, psc = pick(cross)
-    nc, nsc = pick(near + [me])
+                l.append([e, e + 1])
+        return [(qp("pk", 96 * lo, 96 * hi), T.off[:, 6 * lo:6 * hi]) for lo, hi in l]
+    ready, (oc, osc) = [of, qx, qg], qp("own")
+    scales_s = lambda r: S(ready, r[0][1], osc.indirect(r[1]), AF.Copy)
+    scales_v = lambda r: V(ready, "copy", r[0][1], osc.indirect(r[1]))
+    codes = lambda r: V(ready, "copy", w4(r[0][0]), w4(oc).indirect(r[1]))
+    rc, rn = runs(cross), runs(near + [me])
+    psc = [scales_v(r) if i % 2 else scales_s(r) for i, r in enumerate(rc)]
+    pc = [codes(r) for r in rc][-1]
+    nsc = [scales_s(r) for r in rn][-1]
+    nc = [codes(r) for r in rn][-1]
     wait("sync", [nc, nsc])
     k, m = 48 * 2, 96 * me
     for out, in_ in ((by(T.lxnc[:, k:k + 48]), by(T.pkc[:, m:m + 48])), (by(T.lgnc[:, k:k + 48]), by(T.pkc[:, m + 48:m + 96])),
@@ -287,51 +301,45 @@ def rank_program(g, core, T, topo):
             nhop[e], kb = offe[kb:kb + 4], kb + 4
     half = lambda l, i: l[len(l) // 2 * i:len(l) // 2 * (i + 1)]
 
-    wait("gq", [psc])
+    wait("gq", psc)
     fused([(*hop[e], "hsi", T.pks[:, 96 * e:96 * e + 96], T.hds[:]) for e in cross])
     wait("gq", [pc])
     fused([(*hop[e], "hci", by(T.pkc[:, 96 * e:96 * e + 96]), by(T.hdc[:])) for e in cross])
     at = lambda e: 48 * seat(e).index(me)
     two = [(e, i, 96 * e + 48 * i, ("lxn", "lgn")[i]) for e in near for i in range(2)]
-    wait("gq", [nc])
-    fused([(cores[e], half(nhop[e], i), "nco", by(T.pkc[:, p:p + 48]), by(T[b + "c"][:, at(e):at(e) + 48])) for e, i, p, b in two])
     wait("gq", [nsc])
     fused([(cores[e], half(nhop[e], i), "nsc", T.pks[:, p:p + 48], T[b + "s"][:, at(e):at(e) + 48]) for e, i, p, b in two])
-    gid = G([vone], g.affine_select, C("idn"), C("ones"), [[-1, 128]], OP.is_equal, 0.0, 0, 1)
+    wait("gq", [nc])
+    fused([(cores[e], half(nhop[e], i), "nco", by(T.pkc[:, p:p + 48]), by(T[b + "c"][:, at(e):at(e) + 48])) for e, i, p, b in two])
 
+    ie = [S([gid, fe[i]], T.e4[:, 512 * i + i:512 * i + 512:4], C("idn"), AF.Copy) for i in range(4)][-1]
     qw = quant([lw], "ww", 0, 512, T.win[:])
-    ve = V([], "set", T.e4[:], 0.0)
-    vk = V([], "set", T.kt[:], 0.0)
     vl0 = V([], "set", C("la"), 0)
-    vset = None
-    for b in "nc":
-        V([], "set", T["big" + b][:, 2304:2816], 0.0)
-        vset = V([], "set", T["f" + b][:, 48:64], -1.0)
-    ie = None
-    for i in range(4):
-        ie = V([ve, gid], "copy", T.e4[:, 512 * i + i:512 * i + 512:4], C("idn"))
-    qe = quant([ie], "ee", 0, 512, T.e4[:])
+    vset = [V([], "set", T["f" + b][:, 48:64], -1.0) for b in "nc"][-1]
     qpr = quant([lpr], "pp", 0, 128, T.prin[:])
     pp, pps = pickq([qpr, vl0], qp("pq"), qp("pp"), C("la"))
+    fk = [fill(T.kt[:, 0:512]), fill(T.kt[:, 512:544])][-1]
+    foh = [fill(T["big" + b][:, 2304:2816]) for b in "cn"][-1]
+    vrs = S([vz], T.rsw[:], T.zt[:], AF.Identity, bias=128.0)
+    qe = quant([ie], "ee", 0, 512, T.e4[:])
     k1 = V([gip], "ts", C("ka"), C("ip"), 31, None, OP.bitwise_and)
-    k2 = V([k1], "ts", C("kb"), C("ka"), 15, None, OP.bitwise_and)
+    k2 = V([gip], "ts", C("kb"), C("ip"), 15, None, OP.bitwise_and)
+    k3 = V([gip], "ts", C("qi"), C("ip"), 5, None, OP.logical_shift_right)
     kc = V([k1], "copy", C("kcol", 0, 1), C("ka", 0, 1))
     kc2 = V([k1], "ts", C("kcol", 1, 2), C("ka", 0, 1), 32, None, OP.add)
-    w0 = V([kc, gk48], "ts", C("wn", 0, 48), C("kx"), C("kcol", 0, 1), 2.0, OP.is_lt, OP.mult)
-    w1 = V([kc2, gk48], "ts", C("wn", 48, 96), C("kx"), C("kcol", 1, 2), 2.0, OP.is_lt, OP.mult)
-    wm = V([w0, w1], "ts", C("wm"), C("wn"), -1.0, None, OP.add)
-    lo = V([k2], "copy", C("kdol", 0, 2), C("kb", 0, 2))
-    hi = V([k1, k2], "tt", C("kdol", 2, 3), C("ka", 0, 1), C("kb", 0, 1), OP.subtract)
-    hi2 = V([], "set", C("kdol", 3, 4), 32.0)
-    kd, kl = VIEW["kdol"][1], None
-    for a in range(4):
-        p = slice(32 * a, 32 * a + 32)
-        lov, hiv, c = T.kf[p, kd:kd + 2], T.kf[p, kd + 2:kd + 4], 4 * a
-        V([lo, vk], "copy", T.kt[p, c:c + 2], lov)
-        V([lo, vk], "copy", T.kt[p, 16 + c:18 + c], lov)
-        V([hi, hi2, vk], "ts", T.kt[p, 512 + c:514 + c], hiv, 48.0 * a, None, OP.add)
-        kl = V([hi, hi2, vk], "copy", T.kt[p, 528 + c:530 + c], hiv)
-    qk = quant([kl], "kk", 0, 256, T.kt[:])
+    lo = V([k2], "copy", C("klo"), C("kb"))
+    hi = V([k1, k2], "tt", C("kh"), C("ka"), C("kb"), OP.subtract)
+    mk = V([k3, gci], "tt", C("mk"), C("qi"), C("ci"), OP.is_equal)
+    ix = V([k3], "ts", C("kix"), C("qi"), 48.0, 32.0, OP.mult, OP.add)
+    hx = V([hi, k3], "ts", C("khx"), C("qi"), 48.0, C("kh", 0, 1), OP.mult, OP.add)
+    w0 = V([kc, gk48], "ts", C("wn", 0, 48), C("kx"), C("kcol", 0, 1), -2.0, OP.is_equal, OP.mult)
+    w1 = V([kc2, gk48], "ts", C("wn", 48, 96), C("kx"), C("kcol", 1, 2), -2.0, OP.is_equal, OP.mult)
+    wm = V([w0, w1], "ts", C("wm"), C("wn"), 1.0, None, OP.add)
+    kl = None
+    for c, w, d, s in ((0, 8, lo, C("klo", 0, 1)), (1, 8, lo, C("klo", 0, 1)), (32, 4, hx, C("khx", 0, 1)), (33, 4, ix, C("kix", 0, 1)),
+                       (48, 4, hi, C("kh", 0, 1)), (49, 4, mk, 32.0)):
+        kl = V([mk, d, fk], "ts", T.kt[:, c:c + 4 * w - c % 2:4], C("mk", 0, w), s, None, OP.mult)
+    qk = quant([kl], "kk", 0, 136, T.kt[:])
     qu = quant([lu], "uu", 0, 512, T.ubin[:])
 
     ct = V([cum], "tr", C("ctr"), C("cum"))
@@ -346,19 +354,19 @@ def rank_program(g, core, T, topo):
     h3 = V([h2], "tt", C("vae"), C("vad", 0, 16, 2), C("vad", 1, 16, 2), OP.add)
     og1 = V([h3], "copy", T.offg[:, 0:16:2], C("vae"))
     og2 = V([h3], "copy", T.offg[:, 1:16:2], C("vae"))
-    vrs = V([], "set", T.rsw[:], 128.0)
     vcf = V([], "set", C("cf"), 0.0)
     qv = quant([lv], "vv", 0, 128, T.vin[:])
     qzc = quant([vz], "cam", 128, 256, T.zt[:])
 
     R, QUARTERS = {}, range(4)
-    come = {"n": [("nco", 16), ("nsc", 16), ("selfcp", 64)], "c": [("cco", 32), ("csc", 32)]}
+    near_in = [("nco", 16), ("nsc", 16), ("selfcp", 64)]
+    come = {"nf": near_in, "nd": near_in, "cf": [("cxo", 32), ("csc", 32)], "cd": [("cgo", 32), ("csc", 32)]}
     dbank = {"c": (4, 5, 6, 7), "n": (1, 2, 3, 4)}
 
     def products(b, todo):
         for kind, i in todo:
             l, r, o = ("ww", "lx" + b, i) if kind == "f" else ("ee", "lg" + b, dbank[b][i])
-            R[b, kind, i] = MM(come[b] + [qw, qe] + used[o], PS[o][:, 0:192], qp(l, 128 * i, 128 * i + 128), qp(r), True, True)
+            R[b, kind, i] = MM(come[b + kind] + [qw, qe] + used[o], PS[o][:, 0:192], qp(l, 128 * i, 128 * i + 128), qp(r), True, True)
 
     def mask_s(b, i):
         B = T["big" + b]
@@ -386,42 +394,44 @@ def rank_program(g, core, T, topo):
         tn = V(ab, "tr", F[:, 64:128], F[:, 0:64])
 
         def scaled(i):
-            R[b, "x", i] = S([um[i]] + [R[b, "k", j] for j in QUARTERS], B[:, 1536 + i:2304:4], PS[ubank[i]][:, 0:192], AF.Copy, scale=0.0625)
+            deps = [um[i]] + [R[b, "k", j] for j in QUARTERS]
+            out, in_ = B[:, 1536 + i:2304:4], PS[ubank[i]][:, 0:192]
+            R[b, "x", i] = V(deps, "ts", out, in_, 0.0625, None, OP.mult) if i == 3 else S(deps, out, in_, AF.Copy, scale=0.0625)
             used[ubank[i]] = [R[b, "x", i]]
         scaled(0)
         sg = [S([tn], F[:, 256 + 48 * t:304 + 48 * t], F[:, 0:48], AF.Sign, bias=F[:, 64 + 32 * t:65 + 32 * t], scale=-1.0, accum_out=F[:, 160 + t:161 + t]) for t in range(2)]
-        for i in (1, 2, 3):
+        for i in (1, 2):
             scaled(i)
         eq = [V([tn], "ts", B[:, 2816 + 48 * t:2864 + 48 * t], F[:, 0:48], F[:, 64 + 32 * t:65 + 32 * t], None, OP.is_equal) for t in range(2)]
-        em = V(eq + [wm], "tt", B[:, 2912:3008], B[:, 2816:2912], C("wm"), OP.mult)
-        er = [V([em], "red", F[:, 176 + t:177 + t], B[:, 2912 + 48 * t:2960 + 48 * t], AX.X, OP.add) for t in range(2)]
-        rk = V(er + sg, "tt", F[:, 192:194], F[:, 176:178], F[:, 160:162], OP.subtract)
-        oh = [V([rk, gi2, vset], "ts", B[:, 2304 + t:2816:4], C("its"), F[:, 192 + t:193 + t], None, OP.is_equal) for t in range(2)]
+        er = [V([eq[t], wm], "scan", F[:, 352 + 48 * t:400 + 48 * t], B[:, 2816 + 48 * t:2864 + 48 * t], C("wm", 48 * t, 48 * t + 48), 0.0, OP.add, OP.mult) for t in range(2)]
+        oh = [V([er[t], sg[t], gi2, foh], "ts", B[:, 2304 + t:2816:4], C("its"), F[:, 160 + t:161 + t], F[:, 399 + 48 * t:400 + 48 * t], OP.subtract, OP.is_equal) for t in range(2)]
         R[b, "q"] = quant(oh, "oh" + b, 0, 128, B[:, 2304:2816])
+        scaled(3)
 
     def answers(b, o, between):
         po, ll = T["po" + b], T["ll" + b]
         MM([R[b, "q"], qk] + used[o], PS[o][:, 0:128], qp("oh" + b), qp("kk", 0, 128), True, False)
-        lm = MM([], PS[o][:, 0:128], qp("oh" + b), qp("kk", 128, 256), False, True)
+        lm = MM([], PS[o][:, 0:128], qp("oh" + b), qp("kk", 8, 136), False, True)
         between()
+        qd = quant([R[b, "x", i] for i in QUARTERS], "dd" + b, 0, 192, T["big" + b][:, 1536:2304])
         vll = V([lm], "ts", ll[:], PS[o][:, 4:8], 64.0 * me, None, OP.add)
         vpo = V([lm], "copy", po[:], PS[o][:, 0:4])
         used[o] = [vpo, vll]
-        qd = quant([R[b, "x", i] for i in QUARTERS], "dd" + b, 0, 192, T["big" + b][:, 1536:2304])
         rc, rs = pickq([qd, vpo], qp("rr" + b), qp("dd" + b), po[:])
         return qd, vpo, vll, rc, rs
 
-    products("c", (("f", 0), ("f", 2), ("d", 0), ("f", 1), ("d", 1), ("f", 3), ("d", 2), ("d", 3)))
+    products("c", [("f", i) for i in (2, 0, 3, 1)] + [("d", i) for i in QUARTERS])
     for i in (2, 3):
         mask_s("c", i)
+    for i in (0, 1):
+        mask_v("c", i)
     for i in QUARTERS:
-        if i < 2:
-            mask_v("c", i)
         masked("c", i)
     products("n", [("f", i) for i in QUARTERS])
-    strengths("c", 4, (5, 6, 7, 0), lambda: [mask_v("n", i) for i in QUARTERS])
-    products("n", [("d", i) for i in QUARTERS])
-    qdc, poc, llc, rcc, rsc = answers("c", 5, lambda: [masked("n", i) for i in (0, 1)])
+    strengths("c", 4, (5, 6, 7, 0), lambda: [mask_v("n", i) for i in (0, 1, 2)])
+    mask_s("n", 3)
+    products("n", [("d", i) for i in (0, 1)])
+    qdc, poc, llc, rcc, rsc = answers("c", 5, lambda: [products("n", [("d", i) for i in (2, 3)]), masked("n", 0)])
     wait("gq", [llc])
     fused([(*hop[e], "hli", T.llc[:, i:i + 1], T.hrl[:, 0:1]) for i, e in enumerate(cross)])
     wait("gq", [rcc])
@@ -429,7 +439,7 @@ def rank_program(g, core, T, topo):
     wait("gq", [rsc])
     fused([(*hop[e], "hrsi", T.rrcs[:, 16 * i:16 * i + 16], T.hrs[:]) for i, e in enumerate(cross)])
 
-    for i in (2, 3):
+    for i in (1, 2, 3):
         masked("n", i)
     strengths("n", 6, (7, 0, 1, 2), lambda: None)
     qdn, pon, lln, rcn, rsn = answers("n", 3, lambda: None)
@@ -450,7 +460,7 @@ def rank_program(g, core, T, topo):
     gt = V([gg], "tr", T.gt[:], T.gg[:])
     fo = V([gt], "copy", T.fo[:], T.gt[:, 0:256:16])
     arr = [("rcn", 16), ("rsn", 16), ("rcc", 32), ("rsc", 32), qzc, own, owns, fo]
-    zp, zs = pickq(arr, qp("zp"), qp("cam"), T.fo[:])
+    za, zb = [pickq(arr, qp("zp", 128 * h, 128 * h + 128), qp("cam"), T.fo[:, 8 * h:8 * h + 8]) for h in range(2)]
     f1 = V([gt], "ts", C("cfa"), T.gt[:, 0:128:16], 127.5, None, OP.is_lt)
     f2 = V([gt], "ts", C("cfb"), T.gt[:, 128:256:16], 127.5, 2.0, OP.is_lt, OP.mult)
     f3 = V([f1, f2, vcf], "tt", C("cf", 0, 8), C("cfa"), C("cfb"), OP.add)
@@ -459,11 +469,12 @@ def rank_program(g, core, T, topo):
     hf, o = VIEW["cft"][:2]
     g.sync.dma_start(T.ct[:], T[hf][0:8, o:o + 16]).then_inc(T.sem.outs, 16)
     zt = []
-    for i in QUARTERS:
-        l, o = qp("ee", 128 * i, 128 * i + 128), PS[i][:, 0:128]
-        MM([zp, zs] + used[i], o, l, qp("zp", 0, 128), True, False)
-        t = MM([], o, l, qp("zp", 128, 256), False, True)
-        zt.append(V([t], "copy", T.zz[:, i:512:4], o) if i % 2 else S([t], T.zz[:, i:512:4], o, AF.Copy))
+    for h, zh in enumerate((za, zb)):
+        for i in QUARTERS:
+            o = PS[i][:, 0:128]
+            t = MM([*zh] + used[i], o, qp("ee", 128 * i, 128 * i + 128), qp("zp", 128 * h, 128 * h + 128), h == 0, h == 1)
+            if h:
+                zt.append(V([t], "copy", T.zz[:, i:512:4], o) if i % 2 else S([t], T.zz[:, i:512:4], o, AF.Copy))
     zq = quant(zt, "zq", 0, 128, T.zz[:])
     wait("sync", [zq])
     wait("sq", [zq])

@@ -1,13 +1,16 @@
 from concourse.bass import DstId, RemoteDMATransfer
 from concourse.mybir import dt, AluOpType, AxisListType, ActivationFunctionType
 
-OP, AX, AF = AluOpType, AxisListType, ActivationFunctionType
+OP, AF = AluOpType, ActivationFunctionType
 N, CAPP, CAPR = 8, 48, 16
 SIM = 256
 BIG = 9.0e29
 NS = 7
 NV = 16 - NS
 OWN = 130
+
+PLAN = ("cf0 cf1 nT cf2 cf3 nH cs2 cd0 cd1 cd2 nf1 nP ck0 cd3 nf2 ck1 cm0 nd0 cm2 cm1 nf0 cs3 ns2 cm3 nf3 cq nd1 ct nk0 nk1 nd2 ns3 nm0 nm1 nm2 nd3 nm3 "
+        "cu0 cu2 cu1 ca cn cx0 cg cu3 nq ce cx2 cx1 nt cx3 co cz cl nu0 cv na nu2 nn cr nu1 nx0 nu3 ng ne no ny2 nl nx1 ny3 nv nz nO cw nr nw")
 
 F8, U8, U16, BF, F32, I32 = "float8_e4m3fn_x4", "uint8", "uint16", "bfloat16", "float32", "int32"
 SCRATCH = {}
@@ -25,10 +28,10 @@ for _n, _w in dict(st=160, fn=512, fc=512, yo=128).items():
 for _i in range(8):
     SCRATCH["ps%d" % _i] = ("psum", [128, 512], F32)
 VIEW = {}
-for _b, _d, _l in (("ii", I32, "ip8 ic8 ra8 ta8 tb8 ua8 ub8 uc8 ud8 sa8 sb8 sc8 ka8 kb8 kq8 qi8 ci8 ea8 eb8 ec8 ed8 ef8"),
+for _b, _d, _l in (("ii", I32, "ip8 ic8 ra8 jj8 ta8 tb8 ua8 ub8 uc8 sc8 ka8 kb8 kq8 qi8 ci8 eb8 ec8 ed8 ef8"),
                    ("lu", U16, "la8 lb8 lc8 ld8"),
-                   ("kf", F32, "kcol8 klo8 kh8 khx8 kix8 mk8 kthr8 kr16 kk16 nk16 kx48 cse32 rs32"),
-                   ("kb", BF, "vals128 its128 idn128 ones128 wn96 wm96"),
+                   ("kf", F32, "klo8 kh8 khx8 kix8 mk8 kthr8 kr16 kk16 nk16 cse32 rs32"),
+                   ("kb", BF, "vals128 its128 idn128 ones128 wm96"),
                    ("df", F32, "xd32 xo32 va32 vb32 iab64 vab64 vac32 vad16 vae8 xa16 pfa32 pra32 pfb32 prb32 vf40 vr40"),
                    ("db", BF, "fb128 ft128 cum128 ctr128 nla32 nlb32 nra32 nrb32 nl32 nr32 np32"),
                    ("hf", F32, "cf32 cft32 cfa8 cfb8")):
@@ -40,7 +43,7 @@ for _b, _d, _l in (("ii", I32, "ip8 ic8 ra8 ta8 tb8 ua8 ub8 uc8 ud8 sa8 sb8 sc8 
     SCRATCH[_b] = ("sbuf", [128, _o], _d)
 
 SEMAPHORES = ["vq", "sq", "tq", "gq", "ldx", "ldrt", "ldgr", "ldpr", "ldw", "ldu", "ldv", "selfcp", "outs", "outs2", "loc",
-              "hci", "hsi", "hli", "hri", "hrsi", "cxo", "cgo", "csc", "nco", "nsc", "rlc", "rcc", "rsc", "rln", "rcn", "rsn"]
+              "hci", "hsi", "hli", "hri", "hrsi", "cxo", "cgo", "csc", "nxo", "ngo", "nsc", "rlc", "rcc", "rsc", "rln", "rcn", "rsn"]
 
 
 def roads(T, topo):
@@ -129,7 +132,7 @@ def rank_program(g, core, T, topo):
         cnt[q] += 1
         return (q, cnt[q])
 
-    calls = {"copy": g.vector.tensor_copy, "tt": g.vector.tensor_tensor, "ts": g.vector.tensor_scalar, "red": g.vector.tensor_reduce,
+    calls = {"copy": g.vector.tensor_copy, "tt": g.vector.tensor_tensor, "ts": g.vector.tensor_scalar,
              "scan": g.vector.tensor_tensor_scan, "tr": g.vector.transpose, "set": g.vector.memset, "q": g.vector.quantize_mx}
     V = lambda deps, name, *a, **k: run("vq", deps, calls[name], *a, **k)
     S = lambda deps, *a, **k: run("sq", deps, g.scalar.activation, *a, **k)
@@ -161,7 +164,7 @@ def rank_program(g, core, T, topo):
     lx = load(g.sync, "ldx", T.xin[:, 0:512], T.x[:])
     lrt = load(g.scalar, "ldrt", T.rtin[:, 0:32], T.rt[:, 0:32])
     lgr = load(g.sync, "ldgr", T.grin[:, 0:512], T.gr[:])
-    lpr = load(g.scalar, "ldpr", T.prin[:], T.pr[:])
+    lpr = load(g.scalar, "ldpr", T.prin[:, 0:32], T.pr[:, 0:32])
     lw = load(g.sync, "ldw", T.win[:], T.w[:])
     lu = load(g.sync, "ldu", T.ubin[:], T.ub[:])
     lv = load(g.scalar, "ldv", T.vin[:], T.v[:])
@@ -171,54 +174,49 @@ def rank_program(g, core, T, topo):
     gip = G([], g.iota, C("ip"), [[0, 8]], 0, 1)
     gic = G([], g.iota, C("ic"), [[16, 8]], 0, 0)
     gkr = iota("kr", [[1, 16]], 0, 0)
-    gon = iota("ones", [[0, 128]], 1, 0)
-    gid = G([gon], g.affine_select, C("idn"), C("ones"), [[-1, 128]], OP.is_equal, 0.0, 0, 1)
     grm = G([], g.iota, T.rm[:], [[0, 128 * NV]], 1, 0, **flags)
     grm = G([grm], g.iota, T.rm[:, 0:128 * NV:128], [[0, NV]], 0, 0, **flags)
+    gon = iota("ones", [[0, 128]], 1, 0)
+    gid = G([gon], g.affine_select, C("idn"), C("ones"), [[-1, 128]], OP.is_equal, 0.0, 0, 1)
     gva = iota("vals", [[1, 128]], 0, 0)
     gcs = iota("cse", [[0, 4], [64, 8]], -1, 0)
-    gk48 = iota("kx", [[1, 48]], 0, 0)
     gi2 = iota("its", [[0, 8], [-2, 16]], 46, 0)
     gci = G([], g.iota, C("ci"), [[0, 2], [1, 4]], 0, 0)
     vz = V([], "set", T.zt[:], 0.0)
-    vxt = V([], "set", T.xin[:, 512:4 * OWN], 0.0)
-    vr1 = V([], "set", C("rs"), BIG)
-    vs1 = V([], "set", T.st[:, 0:32], 0.0)
-    vs2 = [V([], "set", C(n, 0, 8), 0.0) for n in ("vf", "vr")][1]
     fill = lambda out: S([vz], out, T.zt[:, 0:out.shape[1]], AF.Copy)
     frt = fill(T.rtin[:, 32:512])
     fe = [fill(T.e4[:, 0:512])]
     ra = V([gip], "ts", C("ra"), C("ip"), 15, None, OP.bitwise_and)
+    vr1 = V([], "set", C("rs"), BIG)
+    jj = V([ra, gic], "tt", C("jj"), C("ra"), C("ic"), OP.add)
     vr2 = V([vr1], "set", C("rs", 0, 32, 8), -BIG)
-    ua = V([ra], "ts", C("ua"), C("ra"), 7, None, OP.bitwise_and)
-    sa = V([ra], "ts", C("sa"), C("ra"), 2, None, OP.logical_shift_right)
-    sb = V([gic], "ts", C("sb"), C("ic"), 2, None, OP.logical_shift_right)
-    ea = V([gic], "ts", C("ea"), C("ic"), 16, 2, OP.bitwise_and, OP.logical_shift_right)
-    ta = V([ra], "ts", C("ta"), C("ra"), 3, None, OP.bitwise_and)
-    ub = V([ua], "ts", C("ub"), C("ua"), -2, 7, OP.mult, OP.add)
-    eb = V([ea, sa], "tt", C("eb"), C("ea"), C("sa"), OP.add)
-    tb = V([ta], "ts", C("tb"), C("ta"), 1, None, OP.is_equal)
-    sc = V([sa, sb], "tt", C("sc"), C("sa"), C("sb"), OP.add)
+    eb = V([jj], "ts", C("eb"), C("jj"), 2, 7, OP.logical_shift_right, OP.bitwise_and)
+    ta = V([jj], "ts", C("ta"), C("jj"), 3, None, OP.bitwise_and)
     ec = V([eb], "ts", C("ec"), C("eb"), -2, 7, OP.mult, OP.add)
-    ed = V([ec, tb], "tt", C("ed"), C("ec"), C("tb"), OP.mult)
+    tb = V([ta], "ts", C("tb"), C("ta"), 1, None, OP.is_equal)
     kq = V([gip], "ts", C("kq"), C("ip"), 3, None, OP.bitwise_and)
+    ed = V([ec, tb], "tt", C("ed"), C("ec"), C("tb"), OP.mult)
+    sc = V([jj], "ts", C("sc"), C("jj"), 2, None, OP.logical_shift_right)
     ef = V([ed], "tt", C("ef"), C("ed"), C("eb"), OP.add)
-    uc = V([ub], "tt", C("uc"), C("ub"), C("ra"), OP.add)
-    l1 = V([ef], "copy", C("lb"), C("ef"))
-    ud = V([uc], "tt", C("ud"), C("uc"), C("ic"), OP.add)
     kt = V([kq], "ts", C("kthr"), C("kq"), 16, None, OP.mult)
+    l1 = V([ef], "copy", C("lb"), C("ef"))
     l3 = V([sc], "copy", C("ld"), C("sc"))
-    l2 = V([ud], "copy", C("lc"), C("ud"))
-    kk = V([kt, gkr], "ts", C("kk"), C("kr"), C("kthr", 0, 1), None, OP.add)
-    vgt = V([], "set", T.grin[:, 512:4 * OWN], 0.0)
-    nk = V([kk], "ts", C("nk"), C("kk"), -1.0, -0.5, OP.mult, OP.add)
+    vxt = V([], "set", T.xin[:, 512:4 * OWN], 0.0)
+    vs1 = V([], "set", T.st[:, 0:32], 0.0)
+    kk = S([kt, gkr], C("kk"), C("kr"), AF.Identity, bias=C("kthr", 0, 1))
+    nk = S([kk], C("nk"), C("kk"), AF.Copy, scale=-1.0, bias=-0.5)
 
     qrt = quant([lrt, frt], "rt", 0, 128, T.rtin[:])
     prt, prs = pickq([qrt, l1], qp("rp"), qp("rt"), C("lb"))
-    fe += [fill(T.e4[:, 512 * i:512 * i + 512]) for i in (1, 2, 3)]
     qx = quant([lx, vxt], "own", 0, OWN, T.xin[:])
     ms = MM([prt, prs, qx], PS[0][:, 0:128], qp("rp"), qp("own", 0, 128), True, True)
-    qg = quant([lgr, vgt], "own", OWN, 2 * OWN, T.grin[:])
+    ua = V([jj], "ts", C("ua"), C("jj"), 7, None, OP.bitwise_and)
+    vs2 = [V([], "set", C(n, 0, 8), 0.0) for n in ("vf", "vr")][1]
+    ub = V([ua], "ts", C("ub"), C("ua"), -2, 7, OP.mult, OP.add)
+    uc = V([ub], "tt", C("uc"), C("ub"), C("jj"), OP.add)
+    l2 = V([uc], "copy", C("lc"), C("uc"))
+    fe += [fill(T.e4[:, 512 * i:512 * i + 512]) for i in (1, 2, 3)]
+    fpr = fill(T.prin[:, 32:512])
     tr = V([ms, vs1], "tr", T.st[:, 32:160], PS[0][:, 0:128])
     used[0] = [tr]
     X = [T.st[:, 32 + u:160:4] for u in range(2)]
@@ -244,6 +242,8 @@ def rank_program(g, core, T, topo):
         k = 128 * (r - NS)
         cm = V([cum, kk], "ts", T.cb[:, k:k + 128], C("cum"), C("kk", r, r + 1), None, OP.is_le)
     sn = V([cm, grm], "scan", T.cn[:], T.rm[:], T.cb[:], 0.0, OP.mult, OP.add)
+    vgt = V([], "set", T.grin[:, 512:4 * OWN], 0.0)
+    qg = quant([lgr, vgt], "own", OWN, 2 * OWN, T.grin[:])
     d1 = [V([sn], "copy", C("xd", h + NS, h + 16), T.cn[:, 127:128 * NV:128]) for h in (0, 16)][1]
     xo = V([d1, d2, d3], "tr", C("xo"), C("xd"))
     of = None
@@ -310,157 +310,189 @@ def rank_program(g, core, T, topo):
     wait("gq", [nsc])
     fused([(cores[e], half(nhop[e], i), "nsc", T.pks[:, p:p + 48], T[b + "s"][:, at(e):at(e) + 48]) for e, i, p, b in two])
     wait("gq", [nc])
-    fused([(cores[e], half(nhop[e], i), "nco", by(T.pkc[:, p:p + 48]), by(T[b + "c"][:, at(e):at(e) + 48])) for e, i, p, b in two])
+    for k in range(2):
+        fused([(cores[e], nhop[e], ("nxo", "ngo")[k], by(T.pkc[:, p:p + 48]), by(T[b + "c"][:, at(e):at(e) + 48])) for e, i, p, b in two if i == k])
 
     ie = [S([gid, fe[i]], T.e4[:, 512 * i + i:512 * i + 512:4], C("idn"), AF.Copy) for i in range(4)][-1]
+    o, p = VIEW["wm"][1], VIEW["ones"][1]
+    gwm = gci
+    for a in range(0, 128, 32):
+        gwm = G([gon, gwm], g.affine_select, T.kb[a:a + 32, o:o + 96], T.kb[a:a + 32, p:p + 96], [[32, 2], [-1, 48]], OP.not_equal, -1.0, 0, 1)
     qw = quant([lw], "ww", 0, 512, T.win[:])
+    qe = quant([ie], "ee", 0, 512, T.e4[:])
     vl0 = V([], "set", C("la"), 0)
     vset = [V([], "set", T["f" + b][:, 48:64], -1.0) for b in "nc"][-1]
-    qpr = quant([lpr], "pp", 0, 128, T.prin[:])
+    qpr = quant([lpr, fpr], "pp", 0, 128, T.prin[:])
     pp, pps = pickq([qpr, vl0], qp("pq"), qp("pp"), C("la"))
     fk = [fill(T.kt[:, 0:512]), fill(T.kt[:, 512:544])][-1]
-    foh = [fill(T["big" + b][:, 2304:2816]) for b in "cn"][-1]
+    foh = [fill(T["big" + b][:, 2304:2816]) for b in "nc"][-1]
     vrs = S([vz], T.rsw[:], T.zt[:], AF.Identity, bias=128.0)
-    qe = quant([ie], "ee", 0, 512, T.e4[:])
+    qu = quant([lu], "uu", 0, 512, T.ubin[:])
     k1 = V([gip], "ts", C("ka"), C("ip"), 31, None, OP.bitwise_and)
     k2 = V([gip], "ts", C("kb"), C("ip"), 15, None, OP.bitwise_and)
     k3 = V([gip], "ts", C("qi"), C("ip"), 5, None, OP.logical_shift_right)
-    kc = V([k1], "copy", C("kcol", 0, 1), C("ka", 0, 1))
-    kc2 = V([k1], "ts", C("kcol", 1, 2), C("ka", 0, 1), 32, None, OP.add)
-    lo = V([k2], "copy", C("klo"), C("kb"))
     hi = V([k1, k2], "tt", C("kh"), C("ka"), C("kb"), OP.subtract)
+    lo = V([k2], "copy", C("klo"), C("kb"))
     mk = V([k3, gci], "tt", C("mk"), C("qi"), C("ci"), OP.is_equal)
     ix = V([k3], "ts", C("kix"), C("qi"), 48.0, 32.0, OP.mult, OP.add)
     hx = V([hi, k3], "ts", C("khx"), C("qi"), 48.0, C("kh", 0, 1), OP.mult, OP.add)
-    w0 = V([kc, gk48], "ts", C("wn", 0, 48), C("kx"), C("kcol", 0, 1), -2.0, OP.is_equal, OP.mult)
-    w1 = V([kc2, gk48], "ts", C("wn", 48, 96), C("kx"), C("kcol", 1, 2), -2.0, OP.is_equal, OP.mult)
-    wm = V([w0, w1], "ts", C("wm"), C("wn"), 1.0, None, OP.add)
-    kl = None
-    for c, w, d, s in ((0, 8, lo, C("klo", 0, 1)), (1, 8, lo, C("klo", 0, 1)), (32, 4, hx, C("khx", 0, 1)), (33, 4, ix, C("kix", 0, 1)),
-                       (48, 4, hi, C("kh", 0, 1)), (49, 4, mk, 32.0)):
-        kl = V([mk, d, fk], "ts", T.kt[:, c:c + 4 * w - c % 2:4], C("mk", 0, w), s, None, OP.mult)
-    qk = quant([kl], "kk", 0, 136, T.kt[:])
-    qu = quant([lu], "uu", 0, 512, T.ubin[:])
 
-    ct = V([cum], "tr", C("ctr"), C("cum"))
-    va = V([ct], "ts", C("va"), C("ctr", 0, 128, 4), 49.0, None, OP.min)
-    vb = V([va, gcs], "tt", C("vb"), C("va"), C("cse"), OP.add)
-    ia = V([npn], "ts", C("iab", 0, 32), C("np"), 0.0, None, OP.is_equal)
-    ib = V([npn], "ts", C("iab", 32, 64), C("np"), 1.0, None, OP.is_equal)
-    ma = V([vb, ia], "tt", C("vab", 0, 32), C("vb"), C("iab", 0, 32), OP.mult)
-    mb = V([vb, ib], "tt", C("vab", 32, 64), C("vb"), C("iab", 32, 64), OP.mult)
-    h1 = V([ma, mb], "tt", C("vac"), C("vab", 0, 64, 2), C("vab", 1, 64, 2), OP.add)
-    h2 = V([h1], "tt", C("vad"), C("vac", 0, 32, 2), C("vac", 1, 32, 2), OP.add)
-    h3 = V([h2], "tt", C("vae"), C("vad", 0, 16, 2), C("vad", 1, 16, 2), OP.add)
-    og1 = V([h3], "copy", T.offg[:, 0:16:2], C("vae"))
-    og2 = V([h3], "copy", T.offg[:, 1:16:2], C("vae"))
-    vcf = V([], "set", C("cf"), 0.0)
-    qv = quant([lv], "vv", 0, 128, T.vin[:])
-    qzc = quant([vz], "cam", 128, 256, T.zt[:])
+    R, QUARTERS, free = {}, range(4), list(range(1, 8)) + [0]
 
-    R, QUARTERS = {}, range(4)
-    near_in = [("nco", 16), ("nsc", 16), ("selfcp", 64)]
-    come = {"nf": near_in, "nd": near_in, "cf": [("cxo", 32), ("csc", 32)], "cd": [("cgo", 32), ("csc", 32)]}
-    dbank = {"c": (4, 5, 6, 7), "n": (1, 2, 3, 4)}
+    def tables(b):
+        for c, w, d, s in ((0, 8, lo, C("klo", 0, 1)), (1, 8, lo, C("klo", 0, 1)), (32, 4, hx, C("khx", 0, 1)), (33, 4, ix, C("kix", 0, 1)),
+                           (48, 4, hi, C("kh", 0, 1)), (49, 4, mk, 32.0)):
+            kl = V([mk, d, fk], "ts", T.kt[:, c:c + 4 * w - c % 2:4], C("mk", 0, w), s, None, OP.mult)
+        R["kk"] = quant([kl], "kk", 0, 136, T.kt[:])
+        R["ct"] = V([cum], "tr", C("ctr"), C("cum"))
 
-    def products(b, todo):
-        for kind, i in todo:
-            l, r, o = ("ww", "lx" + b, i) if kind == "f" else ("ee", "lg" + b, dbank[b][i])
-            R[b, kind, i] = MM(come[b + kind] + [qw, qe] + used[o], PS[o][:, 0:192], qp(l, 128 * i, 128 * i + 128), qp(r), True, True)
+    def token_places(b):
+        va = V([R["ct"]], "ts", C("va"), C("ctr", 0, 128, 4), 49.0, None, OP.min)
+        ia = V([npn], "ts", C("iab", 0, 32), C("np"), 0.0, None, OP.is_equal)
+        vb = V([va, gcs], "tt", C("vb"), C("va"), C("cse"), OP.add)
+        ib = V([npn], "ts", C("iab", 32, 64), C("np"), 1.0, None, OP.is_equal)
+        ma = V([vb, ia], "tt", C("vab", 0, 32), C("vb"), C("iab", 0, 32), OP.mult)
+        mb = V([vb, ib], "tt", C("vab", 32, 64), C("vb"), C("iab", 32, 64), OP.mult)
+        h1 = V([ma, mb], "tt", C("vac"), C("vab", 0, 64, 2), C("vab", 1, 64, 2), OP.add)
+        h2 = V([h1], "tt", C("vad"), C("vac", 0, 32, 2), C("vac", 1, 32, 2), OP.add)
+        h3 = V([h2], "tt", C("vae"), C("vad", 0, 16, 2), C("vad", 1, 16, 2), OP.add)
+        R["og"] = [V([h3], "copy", T.offg[:, u:16:2], C("vae")) for u in range(2)]
+
+    def home_tiles(b):
+        R["qv"] = quant([lv], "vv", 0, 128, T.vin[:])
+        R["qz"] = quant([vz], "cam", 128, 256, T.zt[:])
+        R["cf"] = V([], "set", C("cf"), 0.0)
+
+    near_in = [("nsc", 16), ("selfcp", 64)]
+    come = {"nf": near_in + [("nxo", 16)], "nd": near_in + [("ngo", 16)], "cf": [("cxo", 32), ("csc", 32)], "cd": [("cgo", 32), ("csc", 32)]}
+
+    def product(key, deps, l, r, n):
+        o = free.pop(0)
+        R[key] = MM(deps + used[o], PS[o][:, 0:n], l, r, True, True), o
+
+    def give(key, deps):
+        o = R[key][1]
+        used[o] = deps
+        free.append(o)
+
+    def forward(b, i):
+        product((b, "f", i), come[b + "f"] + [qw, qe], qp("ww", 128 * i, 128 * i + 128), qp("lx" + b), 192)
+
+    def unpack(b, i):
+        product((b, "d", i), come[b + "d"] + [qw, qe], qp("ee", 128 * i, 128 * i + 128), qp("lg" + b), 192)
 
     def mask_s(b, i):
-        B = T["big" + b]
+        B, (f, o) = T["big" + b], R[b, "f", i]
         m = B[:, 1536 + 192 * i:1728 + 192 * i]
-        used[i] = [S([R[b, "f", i]], m, PS[i][:, 0:192], AF.Sign)]
-        R[b, "k", i] = S(used[i], B[:, 192 * i:192 * i + 192], m, AF.Relu)
+        s = S([f], m, PS[o][:, 0:192], AF.Sign)
+        give((b, "f", i), [s])
+        R[b, "k", i] = S([s], B[:, 192 * i:192 * i + 192], m, AF.Relu)
 
     def mask_v(b, i):
-        R[b, "k", i] = V([R[b, "f", i]], "ts", T["big" + b][:, 192 * i:192 * i + 192], PS[i][:, 0:192], 0.0, None, OP.is_gt)
-        used[i] = [R[b, "k", i]]
+        f, o = R[b, "f", i]
+        R[b, "k", i] = V([f], "ts", T["big" + b][:, 192 * i:192 * i + 192], PS[o][:, 0:192], 0.0, None, OP.is_gt)
+        give((b, "f", i), [R[b, "k", i]])
 
     def masked(b, i):
-        B, o = T["big" + b], dbank[b][i]
-        R[b, "m", i] = V([R[b, "k", i], R[b, "d", i]], "tt", B[:, 768 + i:1536:4], PS[o][:, 0:192], B[:, 192 * i:192 * i + 192], OP.mult)
-        used[o] = [R[b, "m", i]]
+        B, (d, o) = T["big" + b], R[b, "d", i]
+        R[b, "m", i] = V([R[b, "k", i], d], "tt", B[:, 768 + i:1536:4], PS[o][:, 0:192], B[:, 192 * i:192 * i + 192], OP.mult)
+        give((b, "d", i), [R[b, "m", i]])
 
-    def strengths(b, sbank, ubank, between):
+    def quant_m(b):
+        R[b, "qm"] = quant([R[b, "m", i] for i in QUARTERS], "mm" + b, 0, 192, T["big" + b][:, 768:1536])
+
+    def strengths(b):
+        product((b, "st"), [R[b, "qm"], pp, pps], qp("pq"), qp("mm" + b), 192)
+
+    def before_dx(b, i):
+        product((b, "u", i), [R[b, "qm"], qu], qp("uu", 128 * i, 128 * i + 128), qp("mm" + b), 192)
+
+    def sizes(b):
+        F, (st, o) = T["f" + b], R[b, "st"]
+        R[b, "ab"] = [S([st, vset], F[32 * a:32 * a + 32, 0:48], PS[o][32 * a:32 * a + 32, 48 * a:48 * a + 48], AF.Abs) for a in range(4)]
+        give((b, "st"), R[b, "ab"][-1:])
+
+    def turn(b):
+        F = T["f" + b]
+        R[b, "tn"] = V(R[b, "ab"], "tr", F[:, 64:128], F[:, 0:64])
+
+    def scaled(b, i, on_scalar):
+        B, (u, o) = T["big" + b], R[b, "u", i]
+        deps = [u] + [R[b, "k", j] for j in QUARTERS]
+        out, in_ = B[:, 1536 + i:2304:4], PS[o][:, 0:192]
+        R[b, "x", i] = S(deps, out, in_, AF.Copy, scale=0.0625) if on_scalar else V(deps, "ts", out, in_, 0.0625, None, OP.mult)
+        give((b, "u", i), [R[b, "x", i]])
+
+    def signs(b):
+        F = T["f" + b]
+        R[b, "sg"] = [S([R[b, "tn"]], F[:, 256 + 48 * t:304 + 48 * t], F[:, 0:48], AF.Sign, bias=F[:, 64 + 32 * t:65 + 32 * t], scale=-1.0,
+                        accum_out=F[:, 160 + t:161 + t]) for t in range(2)]
+
+    def equals(b):
         B, F = T["big" + b], T["f" + b]
-        qm = quant([R[b, "m", i] for i in QUARTERS], "mm" + b, 0, 192, B[:, 768:1536])
-        st = MM([qm, pp, pps] + used[sbank], PS[sbank][:, 0:192], qp("pq"), qp("mm" + b), True, True)
-        between()
-        um = [MM([qm, qu] + used[ubank[i]], PS[ubank[i]][:, 0:192], qp("uu", 128 * i, 128 * i + 128), qp("mm" + b), True, True) for i in QUARTERS]
-        ab = [S([st, vset], F[32 * a:32 * a + 32, 0:48], PS[sbank][32 * a:32 * a + 32, 48 * a:48 * a + 48], AF.Abs) for a in range(4)]
-        used[sbank] = ab[-1:]
-        tn = V(ab, "tr", F[:, 64:128], F[:, 0:64])
+        eq = [V([R[b, "tn"]], "ts", B[:, 2816 + 48 * t:2864 + 48 * t], F[:, 0:48], F[:, 64 + 32 * t:65 + 32 * t], None, OP.is_equal) for t in range(2)]
+        R[b, "er"] = [V([eq[t], gwm], "scan", F[:, 352 + 48 * t:400 + 48 * t], B[:, 2816 + 48 * t:2864 + 48 * t], C("wm", 48 * t, 48 * t + 48), 0.0, OP.add, OP.mult)
+                      for t in range(2)]
 
-        def scaled(i):
-            deps = [um[i]] + [R[b, "k", j] for j in QUARTERS]
-            out, in_ = B[:, 1536 + i:2304:4], PS[ubank[i]][:, 0:192]
-            R[b, "x", i] = V(deps, "ts", out, in_, 0.0625, None, OP.mult) if i == 3 else S(deps, out, in_, AF.Copy, scale=0.0625)
-            used[ubank[i]] = [R[b, "x", i]]
-        scaled(0)
-        sg = [S([tn], F[:, 256 + 48 * t:304 + 48 * t], F[:, 0:48], AF.Sign, bias=F[:, 64 + 32 * t:65 + 32 * t], scale=-1.0, accum_out=F[:, 160 + t:161 + t]) for t in range(2)]
-        for i in (1, 2):
-            scaled(i)
-        eq = [V([tn], "ts", B[:, 2816 + 48 * t:2864 + 48 * t], F[:, 0:48], F[:, 64 + 32 * t:65 + 32 * t], None, OP.is_equal) for t in range(2)]
-        er = [V([eq[t], wm], "scan", F[:, 352 + 48 * t:400 + 48 * t], B[:, 2816 + 48 * t:2864 + 48 * t], C("wm", 48 * t, 48 * t + 48), 0.0, OP.add, OP.mult) for t in range(2)]
-        oh = [V([er[t], sg[t], gi2, foh], "ts", B[:, 2304 + t:2816:4], C("its"), F[:, 160 + t:161 + t], F[:, 399 + 48 * t:400 + 48 * t], OP.subtract, OP.is_equal) for t in range(2)]
-        R[b, "q"] = quant(oh, "oh" + b, 0, 128, B[:, 2304:2816])
-        scaled(3)
+    def one_hot(b):
+        B, F = T["big" + b], T["f" + b]
+        oh = [V([R[b, "er"][t], R[b, "sg"][t], gi2, foh], "ts", B[:, 2304 + t:2816:4], C("its"), F[:, 160 + t:161 + t], F[:, 399 + 48 * t:400 + 48 * t],
+                OP.subtract, OP.is_equal) for t in range(2)]
+        R[b, "oh"] = quant(oh, "oh" + b, 0, 128, B[:, 2304:2816])
 
-    def answers(b, o, between):
-        po, ll = T["po" + b], T["ll" + b]
-        MM([R[b, "q"], qk] + used[o], PS[o][:, 0:128], qp("oh" + b), qp("kk", 0, 128), True, False)
-        lm = MM([], PS[o][:, 0:128], qp("oh" + b), qp("kk", 8, 136), False, True)
-        between()
-        qd = quant([R[b, "x", i] for i in QUARTERS], "dd" + b, 0, 192, T["big" + b][:, 1536:2304])
-        vll = V([lm], "ts", ll[:], PS[o][:, 4:8], 64.0 * me, None, OP.add)
-        vpo = V([lm], "copy", po[:], PS[o][:, 0:4])
-        used[o] = [vpo, vll]
-        rc, rs = pickq([qd, vpo], qp("rr" + b), qp("dd" + b), po[:])
-        return qd, vpo, vll, rc, rs
+    def lists(b):
+        o = free.pop(0)
+        MM([R[b, "oh"], R["kk"]] + used[o], PS[o][:, 0:128], qp("oh" + b), qp("kk", 0, 128), True, False)
+        R[b, "l"] = MM([], PS[o][:, 0:128], qp("oh" + b), qp("kk", 8, 136), False, True), o
 
-    products("c", [("f", i) for i in (2, 0, 3, 1)] + [("d", i) for i in QUARTERS])
-    for i in (2, 3):
-        mask_s("c", i)
-    for i in (0, 1):
-        mask_v("c", i)
-    for i in QUARTERS:
-        masked("c", i)
-    products("n", [("f", i) for i in QUARTERS])
-    strengths("c", 4, (5, 6, 7, 0), lambda: [mask_v("n", i) for i in (0, 1, 2)])
-    mask_s("n", 3)
-    products("n", [("d", i) for i in (0, 1)])
-    qdc, poc, llc, rcc, rsc = answers("c", 5, lambda: [products("n", [("d", i) for i in (2, 3)]), masked("n", 0)])
-    wait("gq", [llc])
-    fused([(*hop[e], "hli", T.llc[:, i:i + 1], T.hrl[:, 0:1]) for i, e in enumerate(cross)])
-    wait("gq", [rcc])
-    fused([(*hop[e], "hri", by(T.rrcc[:, 16 * i:16 * i + 16]), by(T.hrc[:])) for i, e in enumerate(cross)])
-    wait("gq", [rsc])
-    fused([(*hop[e], "hrsi", T.rrcs[:, 16 * i:16 * i + 16], T.hrs[:]) for i, e in enumerate(cross)])
+    def quant_dx(b):
+        R[b, "qd"] = quant([R[b, "x", i] for i in QUARTERS], "dd" + b, 0, 192, T["big" + b][:, 1536:2304])
 
-    for i in (1, 2, 3):
-        masked("n", i)
-    strengths("n", 6, (7, 0, 1, 2), lambda: None)
-    qdn, pon, lln, rcn, rsn = answers("n", 3, lambda: None)
-    back = lambda e: 64 + 16 * near_of(e).index(me)
-    ls = lambda e: seat(me).index(e)
-    wait("gq", [lln])
-    fused([(cores[e], nhop[e], "rln", T.lln[:, ls(e):ls(e) + 1], T.lland[:, 4 + near_of(e).index(me):5 + near_of(e).index(me)]) for e in near])
-    wait("gq", [rcn])
-    fused([(cores[e], nhop[e], "rcn", by(T.rrnc[:, 16 * ls(e):16 * ls(e) + 16]), by(T.camc[:, back(e):back(e) + 16])) for e in near])
-    wait("gq", [rsn])
-    fused([(cores[e], nhop[e], "rsn", T.rrns[:, 16 * ls(e):16 * ls(e) + 16], T.cams[:, back(e):back(e) + 16]) for e in near])
-    own, owns = pickq([qdn, pon], qp("cam", 112, 128), qp("ddn"), T.pon[:, 2:3])
+    def entries(b):
+        l, o = R[b, "l"]
+        R[b, "ll"] = V([l], "ts", T["ll" + b][:], PS[o][:, 4:8], 64.0 * me, None, OP.add)
+        R[b, "po"] = V([l], "copy", T["po" + b][:], PS[o][:, 0:4])
+        give((b, "l"), [R[b, "ll"], R[b, "po"]])
+
+    def answers(b):
+        R[b, "rc"], R[b, "rs"] = pickq([R[b, "qd"], R[b, "po"]], qp("rr" + b), qp("dd" + b), T["po" + b][:])
+
+    def own_answers(b):
+        R["own"] = pickq([R[b, "qd"], R[b, "po"]], qp("cam", 112, 128), qp("dd" + b), T["po" + b][:, 2:3])
+
+    def send(b):
+        to, rr, rs, ll = (cross, T.rrcc, T.rrcs, T.llc) if b == "c" else (near, T.rrnc, T.rrns, T.lln)
+        seats = [(e, i) if b == "c" else (e, seat(me).index(e)) for i, e in enumerate(to)]
+        k = lambda e: near_of(e).index(me)
+        for name, hsem, nsem, src, hland, land in (
+                ("ll", "hli", "rln", lambda i: ll[:, i:i + 1], T.hrl[:, 0:1], lambda e: T.lland[:, 4 + k(e):5 + k(e)]),
+                ("rc", "hri", "rcn", lambda i: by(rr[:, 16 * i:16 * i + 16]), by(T.hrc[:]), lambda e: by(T.camc[:, 64 + 16 * k(e):80 + 16 * k(e)])),
+                ("rs", "hrsi", "rsn", lambda i: rs[:, 16 * i:16 * i + 16], T.hrs[:], lambda e: T.cams[:, 64 + 16 * k(e):80 + 16 * k(e)])):
+            wait("gq", [R[b, name]])
+            fused([(*hop[e], hsem, src(i), hland) if b == "c" else (cores[e], nhop[e], nsem, src(i), land(e)) for e, i in seats])
+
+    stage = {"f": forward, "d": unpack, "s": mask_s, "k": mask_v, "m": masked, "q": quant_m, "t": strengths, "u": before_dx, "a": sizes, "n": turn,
+             "x": lambda b, i: scaled(b, i, True), "y": lambda b, i: scaled(b, i, False), "g": signs, "e": equals, "o": one_hot, "l": lists,
+             "z": quant_dx, "v": entries, "r": answers, "w": send, "O": own_answers, "T": tables, "P": token_places, "H": home_tiles}
+    for s in PLAN.split():
+        stage[s[1]](s[0], *[int(i) for i in s[2:]])
+    og1, og2 = R["og"]
+    qv, qzc, vcf, (own, owns), lln = R["qv"], R["qz"], R["cf"], R["own"], R["n", "ll"]
 
     sc1 = V([vrs, lln, gva], "copy", T.rsw[:].indirect(T.lln[:, 2:3]), C("vals", 112, 128))
     sc2 = V([sc1, ("rln", 16)], "copy", T.rsw[:].indirect(T.lland[:, 4:7]), C("vals", 64, 112))
     sc3 = V([sc2, ("rlc", 32)], "copy", T.rsw[:].indirect(T.lland[:, 0:4]), C("vals", 0, 64))
-    gg = V([sc3, og1, og2], "copy", T.gg[:], T.rsw[:].indirect(T.offg[:]))
-    gt = V([gg], "tr", T.gt[:], T.gg[:])
-    fo = V([gt], "copy", T.fo[:], T.gt[:, 0:256:16])
-    arr = [("rcn", 16), ("rsn", 16), ("rcc", 32), ("rsc", 32), qzc, own, owns, fo]
-    za, zb = [pickq(arr, qp("zp", 128 * h, 128 * h + 128), qp("cam"), T.fo[:, 8 * h:8 * h + 8]) for h in range(2)]
+    arr = [("rcn", 16), ("rsn", 16), ("rcc", 32), ("rsc", 32), qzc, own, owns]
+    part = lambda h, w: slice(w * h, w * h + w)
+    gather = lambda h: V([sc3, og1, og2], "copy", T.gg[:, part(h, 128)], T.rsw[:].indirect(T.offg[:, part(h, 8)]))
+    turned = lambda h, d: V([d], "tr", T.gt[:, part(h, 128)], T.gg[:, part(h, 128)])
+    offsets = lambda h, d: V([d], "copy", T.fo[:, part(h, 8)], T.gt[:, 128 * h:128 * h + 128:16])
+    picked = lambda h, d: pickq(arr + [d], qp("zp", 128 * h, 128 * h + 128), qp("cam"), T.fo[:, part(h, 8)])
+    foa = offsets(0, turned(0, gather(0)))
+    gb = gather(1)
+    za = picked(0, foa)
+    gt = turned(1, gb)
+    zb = picked(1, offsets(1, gt))
     f1 = V([gt], "ts", C("cfa"), T.gt[:, 0:128:16], 127.5, None, OP.is_lt)
     f2 = V([gt], "ts", C("cfb"), T.gt[:, 128:256:16], 127.5, 2.0, OP.is_lt, OP.mult)
     f3 = V([f1, f2, vcf], "tt", C("cf", 0, 8), C("cfa"), C("cfb"), OP.add)
@@ -468,11 +500,12 @@ def rank_program(g, core, T, topo):
     wait("sync", [f4])
     hf, o = VIEW["cft"][:2]
     g.sync.dma_start(T.ct[:], T[hf][0:8, o:o + 16]).then_inc(T.sem.outs, 16)
-    zt = []
+    zt, home = [], free[:5]
     for h, zh in enumerate((za, zb)):
         for i in QUARTERS:
-            o = PS[i][:, 0:128]
-            t = MM([*zh] + used[i], o, qp("ee", 128 * i, 128 * i + 128), qp("zp", 128 * h, 128 * h + 128), h == 0, h == 1)
+            b = home[i]
+            o = PS[b][:, 0:128]
+            t = MM([*zh] + used[b], o, qp("ee", 128 * i, 128 * i + 128), qp("zp", 128 * h, 128 * h + 128), h == 0, h == 1)
             if h:
                 zt.append(V([t], "copy", T.zz[:, i:512:4], o) if i % 2 else S([t], T.zz[:, i:512:4], o, AF.Copy))
     zq = quant(zt, "zq", 0, 128, T.zz[:])
@@ -481,8 +514,8 @@ def rank_program(g, core, T, topo):
     g.sync.dma_start(T.oc[:], by(T.zqc[:])).then_inc(T.sem.outs, 16)
     for k in range(4):
         (g.sync if k < 2 else g.scalar).dma_start(T.osc[4 * k:4 * k + 4, :], T.zqs[32 * k:32 * k + 4, :]).then_inc(T.sem["outs" if k < 2 else "outs2"], 16)
-    ym = MM([zq, qv] + used[4], PS[4][:, 0:128], qp("vv"), qp("zq"), True, True)
-    yc = V([ym], "copy", T.yo[:], PS[4][:, 0:128])
+    ym = MM([zq, qv] + used[home[4]], PS[home[4]][:, 0:128], qp("vv"), qp("zq"), True, True)
+    yc = V([ym], "copy", T.yo[:], PS[home[4]][:, 0:128])
     wait("sync", [yc])
     g.sync.dma_start(T.y[:], T.yo[:]).then_inc(T.sem.outs, 16)
 

from concourse.bass import DstId, RemoteDMATransfer
from concourse.mybir import dt, AluOpType, AxisListType, ActivationFunctionType

OP, AF = AluOpType, ActivationFunctionType
N, CAPP, CAPR = 8, 48, 16
SIM = 256
BIG = 9.0e29
NS = 7
NV = 16 - NS
OWN = 130

PLAN = ("cf0 cf1 nT cf2 cf3 nH cs2 cd0 cd1 cd2 nf1 nP ck0 cd3 nf2 ck1 cm0 nd0 cm2 cm1 nf0 cs3 ns2 cm3 nf3 cq nd1 ct nk0 nk1 nd2 ns3 nm0 nm1 nm2 nd3 nm3 "
        "cu0 cu2 cu1 ca cn cx0 cg cu3 nq ce cx2 cx1 nt cx3 co cz cl nu0 cv na nu2 nn cr nu1 nx0 nu3 ng ne no ny2 nl nx1 ny3 nv nz nO cw nr nw")

F8, U8, U16, BF, F32, I32 = "float8_e4m3fn_x4", "uint8", "uint16", "bfloat16", "float32", "int32"
SCRATCH = {}
for _n, _w in dict(xin=4 * OWN, grin=4 * OWN, rtin=512, win=2048, ubin=2048, prin=512, vin=512, zt=512, e4=2048, kt=544,
                   cb=128 * NV, cn=128 * NV, rm=128 * NV, jk=2048, rsw=512, gg=256, gt=256, zz=512, bign=2912, bigc=2912).items():
    SCRATCH[_n] = ("sbuf", [128, _w], BF)
for _n, _w in dict(own=2 * OWN, rt=128, rp=128, ww=512, uu=512, pp=128, pq=128, vv=128, ee=512, kk=136, pk=768, hd=96, hr=16, cam=256,
                   zp=256, zq=128, lxn=192, lgn=192, mmn=192, ddn=192, ohn=128, rrn=64, lxc=192, lgc=192, mmc=192, ddc=192, ohc=128, rrc=64).items():
    SCRATCH[_n + "c"] = ("sbuf", [128, _w], F8)
    SCRATCH[_n + "s"] = ("sbuf", [128, _w], U8)
for _n, _w in dict(off=48, offg=16, fo=16, hrl=2, lland=8, pon=4, poc=4, lln=4, llc=4).items():
    SCRATCH[_n] = ("sbuf", [128, _w], U16)
for _n, _w in dict(st=160, fn=512, fc=512, yo=128).items():
    SCRATCH[_n] = ("sbuf", [128, _w], F32)
for _i in range(8):
    SCRATCH["ps%d" % _i] = ("psum", [128, 512], F32)
VIEW = {}
for _b, _d, _l in (("ii", I32, "ip8 ic8 ra8 jj8 ta8 tb8 ua8 ub8 uc8 sc8 ka8 kb8 kq8 qi8 ci8 eb8 ec8 ed8 ef8"),
                   ("lu", U16, "la8 lb8 lc8 ld8"),
                   ("kf", F32, "klo8 kh8 khx8 kix8 mk8 kthr8 kr16 kk16 nk16 cse32 rs32"),
                   ("kb", BF, "vals128 its128 idn128 ones128 wm96"),
                   ("df", F32, "xd32 xo32 va32 vb32 iab64 vab64 vac32 vad16 vae8 xa16 pfa32 pra32 pfb32 prb32 vf40 vr40"),
                   ("db", BF, "fb128 ft128 cum128 ctr128 nla32 nlb32 nra32 nrb32 nl32 nr32 np32"),
                   ("hf", F32, "cf32 cft32 cfa8 cfb8")):
    _o = 0
    for _t in _l.split():
        _n = _t.rstrip("0123456789")
        VIEW[_n] = (_b, _o, int(_t[len(_n):]))
        _o += int(_t[len(_n):])
    SCRATCH[_b] = ("sbuf", [128, _o], _d)

SEMAPHORES = ["vq", "sq", "tq", "gq", "ldx", "ldrt", "ldgr", "ldpr", "ldw", "ldu", "ldv", "selfcp", "outs", "outs2", "loc",
              "hci", "hsi", "hli", "hri", "hrsi", "cxo", "cgo", "csc", "nxo", "ngo", "nsc", "rlc", "rcc", "rsc", "rln", "rcn", "rsn"]


def roads(T, topo):
    cores = [int(c) for c in T.cores]
    cross = [[e for e in range(N) if e != q and not topo.may_write(cores[q], cores[e])] for q in range(N)]
    road = {}
    for q in range(N):
        for e in cross[q]:
            cq, ce = cores[q], cores[e]
            if topo.die(cq) == topo.die(ce):
                hs = [h for h in topo.cores_of(cq) if h != cq and topo.die(h) == topo.die(cq) and topo.may_write(h, ce)]
                k = [f for f in cross[q] if topo.die(cores[f]) == topo.die(cq)].index(e)
            else:
                hs = [h for h in range(SIM) if topo.mates(h, ce) and topo.die(h) == topo.die(ce) and topo.may_write(cq, h) and topo.may_write(h, ce)]
                k = [s for s in cross[e] if topo.die(cores[s]) != topo.die(ce)].index(q)
            road[(q, e)] = hs[k % len(hs)]
    return cores, cross, road


def bits(es):
    return sum(1 << e for e in es)


def by(v):
    return v.bitcast(dt.uint8)


def w4(v):
    return v.bitcast(dt.uint32)


def hand_on(g, core, T, topo):
    cores, cross, road = roads(T, topo)
    mine = [k for k, h in road.items() if h == core]
    if not mine:
        return
    q, e = mine[0]
    ce = cores[e]
    rid, pid = topo.addr(ce, core)
    es = topo.engines(core, ce)
    al, hs = bits(es), (bits(es[:len(es) // 2]), bits(es[len(es) // 2:]))
    k = cross[e].index(q)
    a = k * CAPP
    g.wait_ge(T.sem.hsi, 4)
    g.remote_dma_fused([RemoteDMATransfer(dst_ids=[DstId(rid=rid, pnc=pid)], dma_engine_mask=m, remote_sem=T.sem.csc, src=s, dst=d)
                        for m, s, d in ((hs[0], T.hds[:, 0:48], T.lxcs[:, a:a + 48]), (hs[1], T.hds[:, 48:96], T.lgcs[:, a:a + 48]))], local_sem=T.sem.loc)
    b = 16 * k
    for sem, rsem, src, to in (("hci", "cxo", by(T.hdc[:, 0:48]), by(T.lxcc[:, a:a + 48])),
                               ("hci", "cgo", by(T.hdc[:, 48:96]), by(T.lgcc[:, a:a + 48])),
                               ("hli", "rlc", T.hrl[:, 0:1], T.lland[:, k:k + 1]),
                               ("hri", "rcc", by(T.hrc[:]), by(T.camc[:, b:b + 16])),
                               ("hrsi", "rsc", T.hrs[:], T.cams[:, b:b + 16])):
        if rsem != "cgo":
            g.wait_ge(T.sem[sem], 4)
        g.remote_dma(to, src, T.sem[rsem], T.sem.loc, pid, rid, al)
    g.wait_ge(T.sem.loc, 6 * len(es))


def rank_program(g, core, T, topo):
    me = T.rank_of(core)
    if me is None:
        return hand_on(g, core, T, topo)
    cores, cross_all, road = roads(T, topo)
    cross = cross_all[me]
    near_of = lambda r: [s for s in range(N) if s != r and s not in cross_all[r]]
    near = near_of(me)
    onchip = lambda a, b: cores[b] in topo.cores_of(cores[a])
    seat = lambda r: near_of(r)[:2] + [r] + near_of(r)[2:]

    eng = {"vq": g.vector, "sq": g.scalar, "tq": g.tensor, "gq": g, "sync": g.sync}
    cnt = {"vq": 0, "sq": 0, "tq": 0, "gq": 0}
    seen = {q: {} for q in eng}

    def wait(q, deps):
        best = {}
        for s, n in deps:
            best[s] = max(best.get(s, 0), n)
        for s, n in best.items():
            if seen[q].get(s, 0) < n:
                eng[q].wait_ge(T.sem[s], n)
                seen[q][s] = n

    def run(q, deps, fn, *a, **k):
        wait(q, deps)
        fn(*a, **k).then_inc(T.sem[q], 1)
        cnt[q] += 1
        return (q, cnt[q])

    calls = {"copy": g.vector.tensor_copy, "tt": g.vector.tensor_tensor, "ts": g.vector.tensor_scalar,
             "scan": g.vector.tensor_tensor_scan, "tr": g.vector.transpose, "set": g.vector.memset, "q": g.vector.quantize_mx}
    V = lambda deps, name, *a, **k: run("vq", deps, calls[name], *a, **k)
    S = lambda deps, *a, **k: run("sq", deps, g.scalar.activation, *a, **k)
    G = lambda deps, fn, *a, **k: run("gq", deps, fn, *a, **k)
    MM = lambda deps, out, l, r, a, b: run("tq", deps, g.tensor.matmul_mx, out, l[0], l[1], r[0], r[1], a, b)
    used = [[] for _ in range(8)]
    PS = [T["ps%d" % i] for i in range(8)]

    def C(n, a=0, b=None, st=1):
        buf, s, w = VIEW[n]
        b = w if b is None else b
        return T[buf][:, s + a:s + b] if st == 1 else T[buf][:, s + a:s + b:st]

    def qp(n, a=0, b=None):
        c, s = T[n + "c"], T[n + "s"]
        b = c.shape[1] if b is None else b
        return c[:, a:b], s[:, a:b]

    def quant(deps, n, a, b, tile):
        c, s = qp(n, a, b)
        return V(deps, "q", c, s, tile)

    def pickq(deps, to, frm, o):
        return V(deps, "copy", w4(to[0]), w4(frm[0]).indirect(o)), S(deps, to[1], frm[1].indirect(o), AF.Copy)

    def load(q, sem, out, in_):
        q.dma_start(out, in_).then_inc(T.sem[sem], 16)
        return (sem, 16)
    lx = load(g.sync, "ldx", T.xin[:, 0:512], T.x[:])
    lrt = load(g.scalar, "ldrt", T.rtin[:, 0:32], T.rt[:, 0:32])
    lgr = load(g.sync, "ldgr", T.grin[:, 0:512], T.gr[:])
    lpr = load(g.scalar, "ldpr", T.prin[:, 0:32], T.pr[:, 0:32])
    lw = load(g.sync, "ldw", T.win[:], T.w[:])
    lu = load(g.sync, "ldu", T.ubin[:], T.ub[:])
    lv = load(g.scalar, "ldv", T.vin[:], T.v[:])

    flags = dict(allow_small_or_imprecise_dtypes=True)
    iota = lambda n, pat, base, cm: G([], g.iota, C(n), pat, base, cm, **flags)
    gip = G([], g.iota, C("ip"), [[0, 8]], 0, 1)
    gic = G([], g.iota, C("ic"), [[16, 8]], 0, 0)
    gkr = iota("kr", [[1, 16]], 0, 0)
    grm = G([], g.iota, T.rm[:], [[0, 128 * NV]], 1, 0, **flags)
    grm = G([grm], g.iota, T.rm[:, 0:128 * NV:128], [[0, NV]], 0, 0, **flags)
    gon = iota("ones", [[0, 128]], 1, 0)
    gid = G([gon], g.affine_select, C("idn"), C("ones"), [[-1, 128]], OP.is_equal, 0.0, 0, 1)
    gva = iota("vals", [[1, 128]], 0, 0)
    gcs = iota("cse", [[0, 4], [64, 8]], -1, 0)
    gi2 = iota("its", [[0, 8], [-2, 16]], 46, 0)
    gci = G([], g.iota, C("ci"), [[0, 2], [1, 4]], 0, 0)
    vz = V([], "set", T.zt[:], 0.0)
    fill = lambda out: S([vz], out, T.zt[:, 0:out.shape[1]], AF.Copy)
    frt = fill(T.rtin[:, 32:512])
    fe = [fill(T.e4[:, 0:512])]
    ra = V([gip], "ts", C("ra"), C("ip"), 15, None, OP.bitwise_and)
    vr1 = V([], "set", C("rs"), BIG)
    jj = V([ra, gic], "tt", C("jj"), C("ra"), C("ic"), OP.add)
    vr2 = V([vr1], "set", C("rs", 0, 32, 8), -BIG)
    eb = V([jj], "ts", C("eb"), C("jj"), 2, 7, OP.logical_shift_right, OP.bitwise_and)
    ta = V([jj], "ts", C("ta"), C("jj"), 3, None, OP.bitwise_and)
    ec = V([eb], "ts", C("ec"), C("eb"), -2, 7, OP.mult, OP.add)
    tb = V([ta], "ts", C("tb"), C("ta"), 1, None, OP.is_equal)
    kq = V([gip], "ts", C("kq"), C("ip"), 3, None, OP.bitwise_and)
    ed = V([ec, tb], "tt", C("ed"), C("ec"), C("tb"), OP.mult)
    sc = V([jj], "ts", C("sc"), C("jj"), 2, None, OP.logical_shift_right)
    ef = V([ed], "tt", C("ef"), C("ed"), C("eb"), OP.add)
    kt = V([kq], "ts", C("kthr"), C("kq"), 16, None, OP.mult)
    l1 = V([ef], "copy", C("lb"), C("ef"))
    l3 = V([sc], "copy", C("ld"), C("sc"))
    vxt = V([], "set", T.xin[:, 512:4 * OWN], 0.0)
    vs1 = V([], "set", T.st[:, 0:32], 0.0)
    kk = S([kt, gkr], C("kk"), C("kr"), AF.Identity, bias=C("kthr", 0, 1))
    nk = S([kk], C("nk"), C("kk"), AF.Copy, scale=-1.0, bias=-0.5)

    qrt = quant([lrt, frt], "rt", 0, 128, T.rtin[:])
    prt, prs = pickq([qrt, l1], qp("rp"), qp("rt"), C("lb"))
    qx = quant([lx, vxt], "own", 0, OWN, T.xin[:])
    ms = MM([prt, prs, qx], PS[0][:, 0:128], qp("rp"), qp("own", 0, 128), True, True)
    ua = V([jj], "ts", C("ua"), C("jj"), 7, None, OP.bitwise_and)
    vs2 = [V([], "set", C(n, 0, 8), 0.0) for n in ("vf", "vr")][1]
    ub = V([ua], "ts", C("ub"), C("ua"), -2, 7, OP.mult, OP.add)
    uc = V([ub], "tt", C("uc"), C("ub"), C("jj"), OP.add)
    l2 = V([uc], "copy", C("lc"), C("uc"))
    fe += [fill(T.e4[:, 512 * i:512 * i + 512]) for i in (1, 2, 3)]
    fpr = fill(T.prin[:, 32:512])
    tr = V([ms, vs1], "tr", T.st[:, 32:160], PS[0][:, 0:128])
    used[0] = [tr]
    X = [T.st[:, 32 + u:160:4] for u in range(2)]
    p1 = [V([tr, vr2], "scan", C(("pfa", "pra")[u]), T.st[:, 28 + u:156:4], C("rs"), 0.0, OP.max, OP.min) for u in range(2)]
    v3 = [V([p1[u], vs2], "tt", C(("vf", "vr")[u], 8, 40), X[u], C(("pfa", "pra")[u]), OP.min) for u in range(2)]
    c1 = V([p1[0]], "tt", C("nla"), C("pfa"), X[0], OP.is_ge)
    c2 = V([p1[1]], "tt", C("nra"), C("pra"), X[1], OP.is_gt)
    p2 = [V([v3[u]], "scan", C(("pfb", "prb")[u]), C(("vf", "vr")[u], 7, 39), C("rs"), 0.0, OP.max, OP.min) for u in range(2)]
    c4 = V([p2[0]], "tt", C("nlb"), C("pfb"), X[0], OP.is_ge)
    c3 = V([p2[1]], "tt", C("nrb"), C("prb"), X[1], OP.is_gt)
    a2 = V([c1, c4], "tt", C("nl"), C("nla"), C("nlb"), OP.add)
    a1 = V([c2, c3], "tt", C("nr"), C("nra"), C("nrb"), OP.add)
    npn = V([a1, a2, l2], "tt", C("np"), C("nr").indirect(C("lc", 0, 2)), C("nl"), OP.add)
    fb = V([npn, l3], "ts", C("fb"), C("np").indirect(C("ld")), 1.5, None, OP.is_lt)
    ft = V([fb], "tr", C("ft"), C("fb"))
    cum = V([ft, vz], "scan", C("cum"), C("ft"), T.zt[:, 0:128], 0.0, OP.add, OP.add)
    sa = None
    for r in range(NS):
        sa = S([cum, nk], T.jk[:, 128 * r:128 * r + 128], C("cum"), AF.Sign, bias=C("nk", r, r + 1), accum_out=C("xa", r, r + 1))
    d2, d3 = [S([sa], C("xd", h, h + NS), C("xa", 0, NS), AF.Copy, scale=-0.5, bias=64.0) for h in (0, 16)]
    cm = None
    for r in range(NS, 16):
        k = 128 * (r - NS)
        cm = V([cum, kk], "ts", T.cb[:, k:k + 128], C("cum"), C("kk", r, r + 1), None, OP.is_le)
    sn = V([cm, grm], "scan", T.cn[:], T.rm[:], T.cb[:], 0.0, OP.mult, OP.add)
    vgt = V([], "set", T.grin[:, 512:4 * OWN], 0.0)
    qg = quant([lgr, vgt], "own", OWN, 2 * OWN, T.grin[:])
    d1 = [V([sn], "copy", C("xd", h + NS, h + 16), T.cn[:, 127:128 * NV:128]) for h in (0, 16)][1]
    xo = V([d1, d2, d3], "tr", C("xo"), C("xd"))
    of = None
    for c in range(3):
        V([xo], "copy", T.off[:, c:48:6], C("xo", c, 32, 4))
        of = V([xo], "ts", T.off[:, 3 + c:48:6], C("xo", c, 32, 4), float(OWN), None, OP.add)

    def runs(es):
        l = []
        for e in sorted(es):
            if l and l[-1][1] == e:
                l[-1][1] = e + 1
            else:
                l.append([e, e + 1])
        return [(qp("pk", 96 * lo, 96 * hi), T.off[:, 6 * lo:6 * hi]) for lo, hi in l]
    ready, (oc, osc) = [of, qx, qg], qp("own")
    scales_s = lambda r: S(ready, r[0][1], osc.indirect(r[1]), AF.Copy)
    scales_v = lambda r: V(ready, "copy", r[0][1], osc.indirect(r[1]))
    codes = lambda r: V(ready, "copy", w4(r[0][0]), w4(oc).indirect(r[1]))
    rc, rn = runs(cross), runs(near + [me])
    psc = [scales_v(r) if i % 2 else scales_s(r) for i, r in enumerate(rc)]
    pc = [codes(r) for r in rc][-1]
    nsc = [scales_s(r) for r in rn][-1]
    nc = [codes(r) for r in rn][-1]
    wait("sync", [nc, nsc])
    k, m = 48 * 2, 96 * me
    for out, in_ in ((by(T.lxnc[:, k:k + 48]), by(T.pkc[:, m:m + 48])), (by(T.lgnc[:, k:k + 48]), by(T.pkc[:, m + 48:m + 96])),
                     (T.lxns[:, k:k + 48], T.pks[:, m:m + 48]), (T.lgns[:, k:k + 48], T.pks[:, m + 48:m + 96])):
        g.sync.dma_start(out, in_).then_inc(T.sem.selfcp, 16)

    offe = topo.engines(core, [cores[e] for e in near if not onchip(me, e)][0])
    one = [x for x in topo.engines(core, [cores[e] for e in near if onchip(me, e)][0]) if x not in offe]
    loc = [0]

    def fused(trs):
        l = []
        for d, es, s, a, b in trs:
            rid, pid = topo.addr(d, core)
            l.append(RemoteDMATransfer(dst_ids=[DstId(rid=rid, pnc=pid)], dma_engine_mask=bits(es), remote_sem=T.sem[s], src=a, dst=b))
            loc[0] += len(es)
        g.remote_dma_fused(l, local_sem=T.sem.loc)

    hop, nhop, ka, kb = {}, {}, 0, 0
    for e in cross:
        h = road[(me, e)]
        if h in topo.cores_of(core):
            hop[e], ka = (h, one[ka:ka + 4]), ka + 4
        else:
            hop[e], kb = (h, offe[kb:kb + 4]), kb + 4
    kb = 0
    for e in near:
        if onchip(me, e):
            nhop[e] = one
        else:
            nhop[e], kb = offe[kb:kb + 4], kb + 4
    half = lambda l, i: l[len(l) // 2 * i:len(l) // 2 * (i + 1)]

    wait("gq", psc)
    fused([(*hop[e], "hsi", T.pks[:, 96 * e:96 * e + 96], T.hds[:]) for e in cross])
    wait("gq", [pc])
    fused([(*hop[e], "hci", by(T.pkc[:, 96 * e:96 * e + 96]), by(T.hdc[:])) for e in cross])
    at = lambda e: 48 * seat(e).index(me)
    two = [(e, i, 96 * e + 48 * i, ("lxn", "lgn")[i]) for e in near for i in range(2)]
    wait("gq", [nsc])
    fused([(cores[e], half(nhop[e], i), "nsc", T.pks[:, p:p + 48], T[b + "s"][:, at(e):at(e) + 48]) for e, i, p, b in two])
    wait("gq", [nc])
    for k in range(2):
        fused([(cores[e], nhop[e], ("nxo", "ngo")[k], by(T.pkc[:, p:p + 48]), by(T[b + "c"][:, at(e):at(e) + 48])) for e, i, p, b in two if i == k])

    ie = [S([gid, fe[i]], T.e4[:, 512 * i + i:512 * i + 512:4], C("idn"), AF.Copy) for i in range(4)][-1]
    o, p = VIEW["wm"][1], VIEW["ones"][1]
    gwm = gci
    for a in range(0, 128, 32):
        gwm = G([gon, gwm], g.affine_select, T.kb[a:a + 32, o:o + 96], T.kb[a:a + 32, p:p + 96], [[32, 2], [-1, 48]], OP.not_equal, -1.0, 0, 1)
    qw = quant([lw], "ww", 0, 512, T.win[:])
    qe = quant([ie], "ee", 0, 512, T.e4[:])
    vl0 = V([], "set", C("la"), 0)
    vset = [V([], "set", T["f" + b][:, 48:64], -1.0) for b in "nc"][-1]
    qpr = quant([lpr, fpr], "pp", 0, 128, T.prin[:])
    pp, pps = pickq([qpr, vl0], qp("pq"), qp("pp"), C("la"))
    fk = [fill(T.kt[:, 0:512]), fill(T.kt[:, 512:544])][-1]
    foh = [fill(T["big" + b][:, 2304:2816]) for b in "nc"][-1]
    vrs = S([vz], T.rsw[:], T.zt[:], AF.Identity, bias=128.0)
    qu = quant([lu], "uu", 0, 512, T.ubin[:])
    k1 = V([gip], "ts", C("ka"), C("ip"), 31, None, OP.bitwise_and)
    k2 = V([gip], "ts", C("kb"), C("ip"), 15, None, OP.bitwise_and)
    k3 = V([gip], "ts", C("qi"), C("ip"), 5, None, OP.logical_shift_right)
    hi = V([k1, k2], "tt", C("kh"), C("ka"), C("kb"), OP.subtract)
    lo = V([k2], "copy", C("klo"), C("kb"))
    mk = V([k3, gci], "tt", C("mk"), C("qi"), C("ci"), OP.is_equal)
    ix = V([k3], "ts", C("kix"), C("qi"), 48.0, 32.0, OP.mult, OP.add)
    hx = V([hi, k3], "ts", C("khx"), C("qi"), 48.0, C("kh", 0, 1), OP.mult, OP.add)

    R, QUARTERS, free = {}, range(4), list(range(1, 8)) + [0]

    def tables(b):
        for c, w, d, s in ((0, 8, lo, C("klo", 0, 1)), (1, 8, lo, C("klo", 0, 1)), (32, 4, hx, C("khx", 0, 1)), (33, 4, ix, C("kix", 0, 1)),
                           (48, 4, hi, C("kh", 0, 1)), (49, 4, mk, 32.0)):
            kl = V([mk, d, fk], "ts", T.kt[:, c:c + 4 * w - c % 2:4], C("mk", 0, w), s, None, OP.mult)
        R["kk"] = quant([kl], "kk", 0, 136, T.kt[:])
        R["ct"] = V([cum], "tr", C("ctr"), C("cum"))

    def token_places(b):
        va = V([R["ct"]], "ts", C("va"), C("ctr", 0, 128, 4), 49.0, None, OP.min)
        ia = V([npn], "ts", C("iab", 0, 32), C("np"), 0.0, None, OP.is_equal)
        vb = V([va, gcs], "tt", C("vb"), C("va"), C("cse"), OP.add)
        ib = V([npn], "ts", C("iab", 32, 64), C("np"), 1.0, None, OP.is_equal)
        ma = V([vb, ia], "tt", C("vab", 0, 32), C("vb"), C("iab", 0, 32), OP.mult)
        mb = V([vb, ib], "tt", C("vab", 32, 64), C("vb"), C("iab", 32, 64), OP.mult)
        h1 = V([ma, mb], "tt", C("vac"), C("vab", 0, 64, 2), C("vab", 1, 64, 2), OP.add)
        h2 = V([h1], "tt", C("vad"), C("vac", 0, 32, 2), C("vac", 1, 32, 2), OP.add)
        h3 = V([h2], "tt", C("vae"), C("vad", 0, 16, 2), C("vad", 1, 16, 2), OP.add)
        R["og"] = [V([h3], "copy", T.offg[:, u:16:2], C("vae")) for u in range(2)]

    def home_tiles(b):
        R["qv"] = quant([lv], "vv", 0, 128, T.vin[:])
        R["qz"] = quant([vz], "cam", 128, 256, T.zt[:])
        R["cf"] = V([], "set", C("cf"), 0.0)

    near_in = [("nsc", 16), ("selfcp", 64)]
    come = {"nf": near_in + [("nxo", 16)], "nd": near_in + [("ngo", 16)], "cf": [("cxo", 32), ("csc", 32)], "cd": [("cgo", 32), ("csc", 32)]}

    def product(key, deps, l, r, n):
        o = free.pop(0)
        R[key] = MM(deps + used[o], PS[o][:, 0:n], l, r, True, True), o

    def give(key, deps):
        o = R[key][1]
        used[o] = deps
        free.append(o)

    def forward(b, i):
        product((b, "f", i), come[b + "f"] + [qw, qe], qp("ww", 128 * i, 128 * i + 128), qp("lx" + b), 192)

    def unpack(b, i):
        product((b, "d", i), come[b + "d"] + [qw, qe], qp("ee", 128 * i, 128 * i + 128), qp("lg" + b), 192)

    def mask_s(b, i):
        B, (f, o) = T["big" + b], R[b, "f", i]
        m = B[:, 1536 + 192 * i:1728 + 192 * i]
        s = S([f], m, PS[o][:, 0:192], AF.Sign)
        give((b, "f", i), [s])
        R[b, "k", i] = S([s], B[:, 192 * i:192 * i + 192], m, AF.Relu)

    def mask_v(b, i):
        f, o = R[b, "f", i]
        R[b, "k", i] = V([f], "ts", T["big" + b][:, 192 * i:192 * i + 192], PS[o][:, 0:192], 0.0, None, OP.is_gt)
        give((b, "f", i), [R[b, "k", i]])

    def masked(b, i):
        B, (d, o) = T["big" + b], R[b, "d", i]
        R[b, "m", i] = V([R[b, "k", i], d], "tt", B[:, 768 + i:1536:4], PS[o][:, 0:192], B[:, 192 * i:192 * i + 192], OP.mult)
        give((b, "d", i), [R[b, "m", i]])

    def quant_m(b):
        R[b, "qm"] = quant([R[b, "m", i] for i in QUARTERS], "mm" + b, 0, 192, T["big" + b][:, 768:1536])

    def strengths(b):
        product((b, "st"), [R[b, "qm"], pp, pps], qp("pq"), qp("mm" + b), 192)

    def before_dx(b, i):
        product((b, "u", i), [R[b, "qm"], qu], qp("uu", 128 * i, 128 * i + 128), qp("mm" + b), 192)

    def sizes(b):
        F, (st, o) = T["f" + b], R[b, "st"]
        R[b, "ab"] = [S([st, vset], F[32 * a:32 * a + 32, 0:48], PS[o][32 * a:32 * a + 32, 48 * a:48 * a + 48], AF.Abs) for a in range(4)]
        give((b, "st"), R[b, "ab"][-1:])

    def turn(b):
        F = T["f" + b]
        R[b, "tn"] = V(R[b, "ab"], "tr", F[:, 64:128], F[:, 0:64])

    def scaled(b, i, on_scalar):
        B, (u, o) = T["big" + b], R[b, "u", i]
        deps = [u] + [R[b, "k", j] for j in QUARTERS]
        out, in_ = B[:, 1536 + i:2304:4], PS[o][:, 0:192]
        R[b, "x", i] = S(deps, out, in_, AF.Copy, scale=0.0625) if on_scalar else V(deps, "ts", out, in_, 0.0625, None, OP.mult)
        give((b, "u", i), [R[b, "x", i]])

    def signs(b):
        F = T["f" + b]
        R[b, "sg"] = [S([R[b, "tn"]], F[:, 256 + 48 * t:304 + 48 * t], F[:, 0:48], AF.Sign, bias=F[:, 64 + 32 * t:65 + 32 * t], scale=-1.0,
                        accum_out=F[:, 160 + t:161 + t]) for t in range(2)]

    def equals(b):
        B, F = T["big" + b], T["f" + b]
        eq = [V([R[b, "tn"]], "ts", B[:, 2816 + 48 * t:2864 + 48 * t], F[:, 0:48], F[:, 64 + 32 * t:65 + 32 * t], None, OP.is_equal) for t in range(2)]
        R[b, "er"] = [V([eq[t], gwm], "scan", F[:, 352 + 48 * t:400 + 48 * t], B[:, 2816 + 48 * t:2864 + 48 * t], C("wm", 48 * t, 48 * t + 48), 0.0, OP.add, OP.mult)
                      for t in range(2)]

    def one_hot(b):
        B, F = T["big" + b], T["f" + b]
        oh = [V([R[b, "er"][t], R[b, "sg"][t], gi2, foh], "ts", B[:, 2304 + t:2816:4], C("its"), F[:, 160 + t:161 + t], F[:, 399 + 48 * t:400 + 48 * t],
                OP.subtract, OP.is_equal) for t in range(2)]
        R[b, "oh"] = quant(oh, "oh" + b, 0, 128, B[:, 2304:2816])

    def lists(b):
        o = free.pop(0)
        MM([R[b, "oh"], R["kk"]] + used[o], PS[o][:, 0:128], qp("oh" + b), qp("kk", 0, 128), True, False)
        R[b, "l"] = MM([], PS[o][:, 0:128], qp("oh" + b), qp("kk", 8, 136), False, True), o

    def quant_dx(b):
        R[b, "qd"] = quant([R[b, "x", i] for i in QUARTERS], "dd" + b, 0, 192, T["big" + b][:, 1536:2304])

    def entries(b):
        l, o = R[b, "l"]
        R[b, "ll"] = V([l], "ts", T["ll" + b][:], PS[o][:, 4:8], 64.0 * me, None, OP.add)
        R[b, "po"] = V([l], "copy", T["po" + b][:], PS[o][:, 0:4])
        give((b, "l"), [R[b, "ll"], R[b, "po"]])

    def answers(b):
        R[b, "rc"], R[b, "rs"] = pickq([R[b, "qd"], R[b, "po"]], qp("rr" + b), qp("dd" + b), T["po" + b][:])

    def own_answers(b):
        R["own"] = pickq([R[b, "qd"], R[b, "po"]], qp("cam", 112, 128), qp("dd" + b), T["po" + b][:, 2:3])

    def send(b):
        to, rr, rs, ll = (cross, T.rrcc, T.rrcs, T.llc) if b == "c" else (near, T.rrnc, T.rrns, T.lln)
        seats = [(e, i) if b == "c" else (e, seat(me).index(e)) for i, e in enumerate(to)]
        k = lambda e: near_of(e).index(me)
        for name, hsem, nsem, src, hland, land in (
                ("ll", "hli", "rln", lambda i: ll[:, i:i + 1], T.hrl[:, 0:1], lambda e: T.lland[:, 4 + k(e):5 + k(e)]),
                ("rc", "hri", "rcn", lambda i: by(rr[:, 16 * i:16 * i + 16]), by(T.hrc[:]), lambda e: by(T.camc[:, 64 + 16 * k(e):80 + 16 * k(e)])),
                ("rs", "hrsi", "rsn", lambda i: rs[:, 16 * i:16 * i + 16], T.hrs[:], lambda e: T.cams[:, 64 + 16 * k(e):80 + 16 * k(e)])):
            wait("gq", [R[b, name]])
            fused([(*hop[e], hsem, src(i), hland) if b == "c" else (cores[e], nhop[e], nsem, src(i), land(e)) for e, i in seats])

    stage = {"f": forward, "d": unpack, "s": mask_s, "k": mask_v, "m": masked, "q": quant_m, "t": strengths, "u": before_dx, "a": sizes, "n": turn,
             "x": lambda b, i: scaled(b, i, True), "y": lambda b, i: scaled(b, i, False), "g": signs, "e": equals, "o": one_hot, "l": lists,
             "z": quant_dx, "v": entries, "r": answers, "w": send, "O": own_answers, "T": tables, "P": token_places, "H": home_tiles}
    for s in PLAN.split():
        stage[s[1]](s[0], *[int(i) for i in s[2:]])
    og1, og2 = R["og"]
    qv, qzc, vcf, (own, owns), lln = R["qv"], R["qz"], R["cf"], R["own"], R["n", "ll"]

    sc1 = V([vrs, lln, gva], "copy", T.rsw[:].indirect(T.lln[:, 2:3]), C("vals", 112, 128))
    sc2 = V([sc1, ("rln", 16)], "copy", T.rsw[:].indirect(T.lland[:, 4:7]), C("vals", 64, 112))
    sc3 = V([sc2, ("rlc", 32)], "copy", T.rsw[:].indirect(T.lland[:, 0:4]), C("vals", 0, 64))
    arr = [("rcn", 16), ("rsn", 16), ("rcc", 32), ("rsc", 32), qzc, own, owns]
    part = lambda h, w: slice(w * h, w * h + w)
    gather = lambda h: V([sc3, og1, og2], "copy", T.gg[:, part(h, 128)], T.rsw[:].indirect(T.offg[:, part(h, 8)]))
    turned = lambda h, d: V([d], "tr", T.gt[:, part(h, 128)], T.gg[:, part(h, 128)])
    offsets = lambda h, d: V([d], "copy", T.fo[:, part(h, 8)], T.gt[:, 128 * h:128 * h + 128:16])
    picked = lambda h, d: pickq(arr + [d], qp("zp", 128 * h, 128 * h + 128), qp("cam"), T.fo[:, part(h, 8)])
    foa = offsets(0, turned(0, gather(0)))
    gb = gather(1)
    za = picked(0, foa)
    gt = turned(1, gb)
    zb = picked(1, offsets(1, gt))
    f1 = V([gt], "ts", C("cfa"), T.gt[:, 0:128:16], 127.5, None, OP.is_lt)
    f2 = V([gt], "ts", C("cfb"), T.gt[:, 128:256:16], 127.5, 2.0, OP.is_lt, OP.mult)
    f3 = V([f1, f2, vcf], "tt", C("cf", 0, 8), C("cfa"), C("cfb"), OP.add)
    f4 = V([f3], "tr", C("cft"), C("cf"))
    wait("sync", [f4])
    hf, o = VIEW["cft"][:2]
    g.sync.dma_start(T.ct[:], T[hf][0:8, o:o + 16]).then_inc(T.sem.outs, 16)
    zt, home = [], free[:5]
    for h, zh in enumerate((za, zb)):
        for i in QUARTERS:
            b = home[i]
            o = PS[b][:, 0:128]
            t = MM([*zh] + used[b], o, qp("ee", 128 * i, 128 * i + 128), qp("zp", 128 * h, 128 * h + 128), h == 0, h == 1)
            if h:
                zt.append(V([t], "copy", T.zz[:, i:512:4], o) if i % 2 else S([t], T.zz[:, i:512:4], o, AF.Copy))
    zq = quant(zt, "zq", 0, 128, T.zz[:])
    wait("sync", [zq])
    wait("sq", [zq])
    g.sync.dma_start(T.oc[:], by(T.zqc[:])).then_inc(T.sem.outs, 16)
    for k in range(4):
        (g.sync if k < 2 else g.scalar).dma_start(T.osc[4 * k:4 * k + 4, :], T.zqs[32 * k:32 * k + 4, :]).then_inc(T.sem["outs" if k < 2 else "outs2"], 16)
    ym = MM([zq, qv] + used[home[4]], PS[home[4]][:, 0:128], qp("vv"), qp("zq"), True, True)
    yc = V([ym], "copy", T.yo[:], PS[home[4]][:, 0:128])
    wait("sync", [yc])
    g.sync.dma_start(T.y[:], T.yo[:]).then_inc(T.sem.outs, 16)

    for s in ("vq", "sq", "tq", "gq"):
        wait("gq", [(s, cnt[s])])
    wait("gq", [lx, lrt, lgr, lw, lpr, lu, lv, ("outs", 80), ("outs2", 32), ("loc", loc[0])])
